import numpy as np
import ml_dtypes


def mxq(x, axis, fmt="e4m3"):
    dtype, down = {"e4m3": (ml_dtypes.float8_e4m3fn, 7), "e5m2": (ml_dtypes.float8_e5m2, 14)}[fmt]
    v = np.moveaxis(np.asarray(x, np.float32).astype(ml_dtypes.bfloat16).astype(np.float64), axis, -1)
    blocks = v.reshape(v.shape[:-1] + (-1, 32))
    amax = np.abs(blocks).max(-1, keepdims=True)
    byte = np.maximum(np.where(amax > 0, np.frexp(amax)[1] - 1 + 127, 0) - down, 1)
    scale = np.exp2(byte - 127.0)
    codes = (blocks / scale).astype(np.float32).astype(dtype).astype(np.float64)
    return np.moveaxis((codes * scale).reshape(v.shape), -1, axis)


WIDE = False


def mx_kscale(k):
    if not WIDE:
        return np.ones(k)
    levels = np.array([10, -10, 5, -5, 0])
    if k % 512:
        return np.exp2(np.random.permutation(np.resize(levels, k // 32))).repeat(32)
    a = np.empty((k // 512, 16))
    for p in range(k // 512):
        a[p, :8] = np.random.permutation(np.resize(levels, 8))
        for g in range(8):
            far = levels[np.abs(levels - a[p, g]) >= 10]
            a[p, g + 8] = far[np.random.randint(len(far))]
    return np.exp2(a.ravel()).repeat(32)


def f64(x):
    return np.asarray(x).astype(np.float64)


def striped(idx):
    return np.tile(idx.reshape(-1, 16).T, (8, 1)).astype(np.uint16)


def unstriped(offs):
    return offs[:16].T.reshape(-1).astype(np.int64)


E2M1 = np.array([0.0, 0.5, 1.0, 1.5, 2.0, 3.0, 4.0, 6.0, -0.0, -0.5, -1.0, -1.5, -2.0, -3.0, -4.0, -6.0])


def pack_weight(w, fmt):
    k, n = w.shape
    w = f64(np.asarray(w, np.float32).astype(ml_dtypes.bfloat16)).reshape(k // 32, 32, n)
    amax = np.abs(w).max(1)
    if fmt == "e4m3":
        byte = np.frexp(amax)[1] - 1 + 127 - 7
    else:
        mant, ex = np.frexp(amax / 6.0)
        byte = np.where(mant > 0.5, ex, ex - 1) + 127
    byte = np.clip(np.where(amax > 0, byte, 1), 1, 254)
    scaled = (w * np.exp2(127.0 - byte)[:, None, :]).reshape(k, n).astype(np.float32)
    by_word = np.ascontiguousarray(scaled.reshape(k // 512, 128, 4, n).transpose(0, 1, 3, 2))
    if fmt == "e4m3":
        words = by_word.astype(ml_dtypes.float8_e4m3fn).view(np.uint8)
    else:
        c = by_word.astype(ml_dtypes.float4_e2m1fn).view(np.uint8) & 0xF
        words = (c[..., 0::2] | (c[..., 1::2] << 4)).reshape(k // 512, 128, 2 * n)
    return np.ascontiguousarray(words), np.ascontiguousarray(byte.astype(np.uint8).reshape(k // 512, 16, n))


def unpack_weight(words, scales, fmt):
    g, _, n = scales.shape
    words = np.ascontiguousarray(words).reshape(g, 128, n, -1)
    if fmt == "e4m3":
        vals = words.view(ml_dtypes.float8_e4m3fn).astype(np.float64)
    else:
        nib = np.empty((g, 128, n, 4), np.uint8)
        nib[..., 0::2] = words & 0xF
        nib[..., 1::2] = words >> 4
        vals = E2M1[nib]
    vals = vals * np.repeat(np.exp2(scales.astype(np.float64) - 127.0), 8, axis=1)[..., None]
    return vals.transpose(0, 1, 3, 2).reshape(g * 512, n)


K, T, E, C, N = 2560, 2048, 6, 256, 128


def by_expert(wq, xq):
    return np.concatenate([wq[e].T @ xq[:, e * C:(e + 1) * C] for e in range(E)], axis=1)


def setup_inputs():
    n = np.random.standard_normal
    s = mx_kscale(K)[:, None]
    x = pack_weight(n((K, T)) * s, "e4m3")
    return {
        "x_words": x[0],
        "x_scales": x[1],
        "w": (n((E + 1, K, N)) / np.sqrt(K) / s[None]).astype(np.float32),
        "b": (0.3 * n((N, E + 1))).astype(np.float32),
        "gate": np.tile(np.random.uniform(0.2, 1.0, E * C), (N, 1)).astype(np.float32),
        "offs": striped(np.random.permutation(T)[:E * C]),
    }


def reference(x_words, x_scales, w, b, gate, offs):
    idx = unstriped(offs)
    wq = mxq(f64(w), 1, "e4m3")
    xs = unpack_weight(x_words, x_scales, "e4m3")
    ys = (wq[E].T @ xs) + f64(b)[:, E:]
    xq = unpack_weight(x_words, x_scales, "e4m3")[:, idx]
    y = by_expert(wq, xq)
    y = y + np.repeat(f64(b)[:, :E], C, axis=1)
    out = ys
    out[:, idx] += f64(gate) * y
    return out

@@ -1,0 +1,206 @@
+from contextlib import ExitStack
+
+import concourse.mybir as mybir
+from concourse.masks import make_identity
+
+K, T, E, C, N = 2560, 2048, 6, 256, 128
+SLOTS = E * C
+FLOPS = 2 * K * N * (T + SLOTS)
+
+F32 = mybir.dt.float32
+BF16 = mybir.dt.bfloat16
+I32 = mybir.dt.int32
+U32 = mybir.dt.uint32
+U16 = mybir.dt.uint16
+U8 = mybir.dt.uint8
+FP8X4 = mybir.dt.float8_e4m3fn_x4
+ADD = mybir.AluOpType.add
+MULT = mybir.AluOpType.mult
+IDENTITY = mybir.ActivationFunctionType.Identity
+
+P = 128
+PACK = 4
+K_PASS = P * PACK
+PASSES = K // K_PASS
+BANK = 512
+LAST = PASSES - 1
+GATE_ROW = SLOTS // P
+
+
+def tile_moe_shr_lin_bias_kernel(tc, x_words, x_scales, w, b, gate, offs, out):
+    nc = tc.nc
+    w_rows = w.rearrange("e k n -> (e k) n")
+
+    with ExitStack() as ctx:
+        keep = ctx.enter_context(tc.tile_pool(name="keep", bufs=1))
+        cast_pool = ctx.enter_context(tc.tile_pool(name="cast", bufs=10))
+        psum_shared = ctx.enter_context(tc.psum_pool(name="psum_shared", bufs=1))
+        psum_ring = ctx.enter_context(tc.psum_pool(name="psum_ring", bufs=4))
+
+        offsets = keep.tile([P, SLOTS // 16], U16, name="offsets")
+        nc.sync.dma_start(offsets[:], offs)
+
+        token_scales = keep.tile([P, T], U8, name="token_scales", align_bytes=64)
+        token_scales_last = keep.tile([P, T], U8, name="token_scales_last", align_bytes=64)
+        slot_scales = keep.tile([P, SLOTS], U8, name="slot_scales", align_bytes=64)
+        slot_scales_last = keep.tile([P, SLOTS], U8, name="slot_scales_last", align_bytes=64)
+        routed = keep.tile([P, T], F32, name="routed")
+        nc.vector.memset(token_scales[:].bitcast(I32), 0)
+        nc.vector.memset(token_scales_last[:].bitcast(I32), 0)
+        nc.vector.memset(slot_scales_last[:].bitcast(I32), 0)
+        nc.vector.memset(routed[:], 0.0)
+
+        for q in range(4):
+            nc.scalar.dma_start(
+                token_scales[32 * q : 32 * q + 4 * PASSES, :].bitcast(I32),
+                x_scales[:, 4 * q : 4 * q + 4, :].bitcast(I32),
+            )
+
+        token_words = [keep.tile([P, T], U32, name="token_words%d" % o, align_bytes=64) for o in range(PASSES)]
+        slot_words = [keep.tile([P, SLOTS], U32, name="slot_words%d" % o, align_bytes=64) for o in range(LAST)]
+        slot_words_last = [keep.tile([P, 2 * C], U32, name="slot_words_last%d" % i, align_bytes=64) for i in range(E // 2)]
+
+        def load_tokens(o):
+            nc.sync.dma_start(token_words[o][:].bitcast(I32), x_words[o].rearrange("p t r -> p (t r)").bitcast(I32))
+
+        def gather_tokens(o):
+            if o < LAST:
+                nc.vector.tensor_copy(slot_words[o][:], token_words[o][:].indirect(offsets[:]))
+            else:
+                for i in range(E // 2):
+                    nc.vector.tensor_copy(slot_words_last[i][:], token_words[o][:].indirect(offsets[:, 32 * i : 32 * i + 32]))
+
+        w_codes = {}
+        w_scales = {}
+
+        def weights(first, count):
+            raw = keep.tile([P, 2, PACK, N], F32, name="raw%d" % first, tag="raw%d" % first)
+            nc.sync.dma_start(
+                raw[:, :count],
+                w_rows[first * K_PASS : (first + count) * K_PASS, :].rearrange("(u p j) n -> p u j n", p=P, j=PACK),
+            )
+            grouped = cast_pool.tile([P, 2, N, PACK], BF16, name="grouped", align_bytes=64)
+            nc.scalar.copy(
+                grouped[:, :count].rearrange("p u (c i) j -> p u c j i", i=4),
+                raw[:, :count].rearrange("p u j (c i) -> p u c j i", i=4),
+            )
+            codes = keep.tile([P, count * N], U32, name="codes%d" % first, align_bytes=64)
+            scales = keep.tile([P, count * N], U8, name="scales%d" % first, align_bytes=64)
+            nc.vector.quantize_mx(codes[:].bitcast(FP8X4), scales[:], grouped[:, :count].rearrange("p u n j -> p (u n j)"))
+            for u in range(count):
+                w_codes[first + u] = codes[:, u * N : (u + 1) * N]
+                w_scales[first + u] = scales[:, u * N : (u + 1) * N]
+
+        shared = [psum_shared.tile([P, BANK], F32, name="shared%d" % i) for i in range(T // BANK)]
+
+        def shared_pass(o):
+            for i in range(T // BANK):
+                cols = slice(i * BANK, (i + 1) * BANK)
+                plane = token_scales[4 * o :, cols] if o < LAST else token_scales_last[:, cols]
+                nc.tensor.matmul_mx(
+                    shared[i][:],
+                    lhsT=w_codes[E * PASSES + o].bitcast(FP8X4),
+                    lhsT_scale=w_scales[E * PASSES + o],
+                    rhs=token_words[o][:, cols].bitcast(FP8X4),
+                    rhs_scale=plane,
+                    start=(o == 0),
+                    stop=(o == LAST),
+                )
+
+        bias = keep.tile([P, E + 1], F32, name="bias")
+        gate_all = keep.tile([P, SLOTS], F32, name="gate_all")
+
+        def spread_gate():
+            gate_row = keep.tile([P, GATE_ROW], F32, name="gate_row")
+            nc.sync.dma_start(gate_row[:], gate[0].rearrange("(p m) -> p m", m=GATE_ROW))
+            nc.sync.dma_start(bias[:], b)
+            identity = keep.tile([P, P], F32, name="identity")
+            make_identity(nc, identity[:])
+            by_column = gate_all[:].rearrange("q (p m) -> q p m", m=GATE_ROW)
+            for g in range(GATE_ROW // 4):
+                bank = psum_ring.tile([P, 4, P], F32, name="bank")
+                for r in range(4):
+                    m = 4 * g + r
+                    nc.tensor.transpose(bank[:, r, :], gate_row[:, m : m + 1].to_broadcast([P, P]), identity[:])
+                nc.scalar.copy(by_column[:, :, 4 * g : 4 * g + 4], bank[:].rearrange("q r p -> q p r"))
+
+        def expert(e, reuse):
+            slots = slice(e * C, (e + 1) * C)
+            bank = psum_ring.tile([P, 4, P], F32, name="bank")
+            acc = bank[:].rearrange("q r p -> q (r p)")[:, :C]
+            for o in range(PASSES):
+                if o < LAST:
+                    words, plane = slot_words[o][:, slots], slot_scales[4 * o :, slots]
+                else:
+                    words, plane = slot_words_last[e // 2][:, (e % 2) * C : (e % 2 + 1) * C], slot_scales_last[:, slots]
+                nc.tensor.matmul_mx(
+                    acc,
+                    lhsT=w_codes[e * PASSES + o].bitcast(FP8X4),
+                    lhsT_scale=w_scales[e * PASSES + o],
+                    rhs=words.bitcast(FP8X4),
+                    rhs_scale=plane,
+                    start=(o == 0),
+                    stop=(o == LAST),
+                )
+            y = keep.tile([P, C], F32, name="y%d" % e, tag="raw%d" % reuse)
+            nc.scalar.activation(y[:], acc, IDENTITY, bias=bias[:, e : e + 1])
+            nc.vector.tensor_tensor(routed[:].indirect(offsets[:, 16 * e : 16 * e + 16]), y[:], gate_all[:, slots], MULT)
+
+        first_shared = E * PASSES
+        load_tokens(0)
+        nc.vector.tensor_copy(slot_scales[:], token_scales[:].indirect(offsets[:]))
+        gather_tokens(0)
+        weights(first_shared, 2)
+        weights(0, 2)
+        shared_pass(0)
+        spread_gate()
+        load_tokens(1)
+        gather_tokens(1)
+        shared_pass(1)
+        weights(2, 2)
+        weights(4, 2)
+        load_tokens(2)
+        gather_tokens(2)
+        for q in range(4):
+            nc.sync.dma_start(
+                slot_scales_last[32 * q : 32 * q + 4, :].bitcast(I32),
+                slot_scales[32 * q + 16 : 32 * q + 20, :].bitcast(I32),
+            )
+        weights(6, 2)
+        weights(first_shared + 2, 2)
+        shared_pass(2)
+        load_tokens(3)
+        gather_tokens(3)
+        shared_pass(3)
+        for q in range(4):
+            nc.sync.dma_start(
+                token_scales_last[32 * q : 32 * q + 4, :].bitcast(I32),
+                x_scales[LAST, 4 * q : 4 * q + 4, :].bitcast(I32),
+            )
+        weights(8, 2)
+        weights(10, 2)
+        load_tokens(4)
+        gather_tokens(4)
+        weights(12, 2)
+        weights(14, 2)
+        weights(16, 2)
+        expert(0, 14)
+        expert(1, 16)
+        weights(first_shared + 4, 1)
+        shared_pass(4)
+        weights(18, 2)
+        weights(20, 2)
+        expert(2, 20)
+        weights(22, 2)
+        weights(24, 2)
+        expert(3, 24)
+        weights(26, 2)
+        weights(28, 2)
+        expert(4, 26)
+        expert(5, 28)
+
+        for i in range(T // BANK):
+            cols = slice(i * BANK, (i + 1) * BANK)
+            result = keep.tile([P, BANK], F32, name="result%d" % i)
+            nc.vector.scalar_tensor_tensor(result[:], shared[i][:], bias[:, E : E + 1], routed[:, cols], ADD, ADD)
+            nc.sync.dma_start(out[:, cols], result[:])

@@ -25,6 +25,7 @@ PASSES = K // K_PASS
 BANK = 512
 LAST = PASSES - 1
 GATE_ROW = SLOTS // P
+HEAD = 2
 
 
 def tile_moe_shr_lin_bias_kernel(tc, x_words, x_scales, w, b, gate, offs, out):
@@ -33,7 +34,7 @@ def tile_moe_shr_lin_bias_kernel(tc, x_words, x_scales, w, b, gate, offs, out):
 
     with ExitStack() as ctx:
         keep = ctx.enter_context(tc.tile_pool(name="keep", bufs=1))
-        cast_pool = ctx.enter_context(tc.tile_pool(name="cast", bufs=10))
+        cast_pool = ctx.enter_context(tc.tile_pool(name="cast", bufs=5))
         psum_shared = ctx.enter_context(tc.psum_pool(name="psum_shared", bufs=1))
         psum_ring = ctx.enter_context(tc.psum_pool(name="psum_ring", bufs=4))
 
@@ -50,15 +51,10 @@ def tile_moe_shr_lin_bias_kernel(tc, x_words, x_scales, w, b, gate, offs, out):
         nc.vector.memset(slot_scales_last[:].bitcast(I32), 0)
         nc.vector.memset(routed[:], 0.0)
 
-        for q in range(4):
-            nc.scalar.dma_start(
-                token_scales[32 * q : 32 * q + 4 * PASSES, :].bitcast(I32),
-                x_scales[:, 4 * q : 4 * q + 4, :].bitcast(I32),
-            )
-
         token_words = [keep.tile([P, T], U32, name="token_words%d" % o, align_bytes=64) for o in range(PASSES)]
         slot_words = [keep.tile([P, SLOTS], U32, name="slot_words%d" % o, align_bytes=64) for o in range(LAST)]
-        slot_words_last = [keep.tile([P, 2 * C], U32, name="slot_words_last%d" % i, align_bytes=64) for i in range(E // 2)]
+        slot_words_head = keep.tile([P, HEAD * C], U32, name="slot_words_head", align_bytes=64)
+        slot_words_tail = keep.tile([P, (E - HEAD) * C], U32, name="slot_words_tail", align_bytes=64)
 
         def load_tokens(o):
             nc.sync.dma_start(token_words[o][:].bitcast(I32), x_words[o].rearrange("p t r -> p (t r)").bitcast(I32))
@@ -67,29 +63,34 @@ def tile_moe_shr_lin_bias_kernel(tc, x_words, x_scales, w, b, gate, offs, out):
             if o < LAST:
                 nc.vector.tensor_copy(slot_words[o][:], token_words[o][:].indirect(offsets[:]))
             else:
-                for i in range(E // 2):
-                    nc.vector.tensor_copy(slot_words_last[i][:], token_words[o][:].indirect(offsets[:, 32 * i : 32 * i + 32]))
+                nc.vector.tensor_copy(slot_words_head[:], token_words[o][:].indirect(offsets[:, : 16 * HEAD]))
+                nc.vector.tensor_copy(slot_words_tail[:], token_words[o][:].indirect(offsets[:, 16 * HEAD :]))
 
         w_codes = {}
         w_scales = {}
 
-        def weights(first, count):
+        grouped = {}
+
+        def load_weights(first, count, group):
             raw = keep.tile([P, 2, PACK, N], F32, name="raw%d" % first, tag="raw%d" % first)
             nc.sync.dma_start(
                 raw[:, :count],
                 w_rows[first * K_PASS : (first + count) * K_PASS, :].rearrange("(u p j) n -> p u j n", p=P, j=PACK),
             )
-            grouped = cast_pool.tile([P, 2, N, PACK], BF16, name="grouped", align_bytes=64)
+            if first == group:
+                grouped[group] = cast_pool.tile([P, 4, N, PACK], BF16, name="grouped", align_bytes=64)
             nc.scalar.copy(
-                grouped[:, :count].rearrange("p u (c i) j -> p u c j i", i=4),
+                grouped[group][:, first - group : first - group + count].rearrange("p u (c i) j -> p u c j i", i=4),
                 raw[:, :count].rearrange("p u j (c i) -> p u c j i", i=4),
             )
-            codes = keep.tile([P, count * N], U32, name="codes%d" % first, align_bytes=64)
-            scales = keep.tile([P, count * N], U8, name="scales%d" % first, align_bytes=64)
-            nc.vector.quantize_mx(codes[:].bitcast(FP8X4), scales[:], grouped[:, :count].rearrange("p u n j -> p (u n j)"))
+
+        def quantize_weights(group, count):
+            codes = keep.tile([P, count * N], U32, name="codes%d" % group, align_bytes=64)
+            scales = keep.tile([P, count * N], U8, name="scales%d" % group, align_bytes=64)
+            nc.vector.quantize_mx(codes[:].bitcast(FP8X4), scales[:], grouped[group][:, :count].rearrange("p u n j -> p (u n j)"))
             for u in range(count):
-                w_codes[first + u] = codes[:, u * N : (u + 1) * N]
-                w_scales[first + u] = scales[:, u * N : (u + 1) * N]
+                w_codes[group + u] = codes[:, u * N : (u + 1) * N]
+                w_scales[group + u] = scales[:, u * N : (u + 1) * N]
 
         shared = [psum_shared.tile([P, BANK], F32, name="shared%d" % i) for i in range(T // BANK)]
 
@@ -113,7 +114,6 @@ def tile_moe_shr_lin_bias_kernel(tc, x_words, x_scales, w, b, gate, offs, out):
         def spread_gate():
             gate_row = keep.tile([P, GATE_ROW], F32, name="gate_row")
             nc.sync.dma_start(gate_row[:], gate[0].rearrange("(p m) -> p m", m=GATE_ROW))
-            nc.sync.dma_start(bias[:], b)
             identity = keep.tile([P, P], F32, name="identity")
             make_identity(nc, identity[:])
             by_column = gate_all[:].rearrange("q (p m) -> q p m", m=GATE_ROW)
@@ -124,15 +124,17 @@ def tile_moe_shr_lin_bias_kernel(tc, x_words, x_scales, w, b, gate, offs, out):
                     nc.tensor.transpose(bank[:, r, :], gate_row[:, m : m + 1].to_broadcast([P, P]), identity[:])
                 nc.scalar.copy(by_column[:, :, 4 * g : 4 * g + 4], bank[:].rearrange("q r p -> q p r"))
 
-        def expert(e, reuse):
+        def expert(e, y):
             slots = slice(e * C, (e + 1) * C)
             bank = psum_ring.tile([P, 4, P], F32, name="bank")
             acc = bank[:].rearrange("q r p -> q (r p)")[:, :C]
             for o in range(PASSES):
                 if o < LAST:
                     words, plane = slot_words[o][:, slots], slot_scales[4 * o :, slots]
+                elif e < HEAD:
+                    words, plane = slot_words_head[:, slots], slot_scales_last[:, slots]
                 else:
-                    words, plane = slot_words_last[e // 2][:, (e % 2) * C : (e % 2 + 1) * C], slot_scales_last[:, slots]
+                    words, plane = slot_words_tail[:, (e - HEAD) * C : (e - HEAD + 1) * C], slot_scales_last[:, slots]
                 nc.tensor.matmul_mx(
                     acc,
                     lhsT=w_codes[e * PASSES + o].bitcast(FP8X4),
@@ -142,33 +144,57 @@ def tile_moe_shr_lin_bias_kernel(tc, x_words, x_scales, w, b, gate, offs, out):
                     start=(o == 0),
                     stop=(o == LAST),
                 )
-            y = keep.tile([P, C], F32, name="y%d" % e, tag="raw%d" % reuse)
-            nc.scalar.activation(y[:], acc, IDENTITY, bias=bias[:, e : e + 1])
-            nc.vector.tensor_tensor(routed[:].indirect(offsets[:, 16 * e : 16 * e + 16]), y[:], gate_all[:, slots], MULT)
+            nc.scalar.activation(y, acc, IDENTITY, bias=bias[:, e : e + 1])
 
-        first_shared = E * PASSES
+        def experts(first, count, reuse):
+            y = keep.tile([P, count * C], F32, name="y%d" % first, tag="raw%d" % reuse)
+            for i in range(count):
+                expert(first + i, y[:, i * C : (i + 1) * C])
+            nc.vector.tensor_tensor(
+                routed[:].indirect(offsets[:, 16 * first : 16 * (first + count)]),
+                y[:],
+                gate_all[:, first * C : (first + count) * C],
+                MULT,
+            )
+
+        sh = E * PASSES
         load_tokens(0)
-        nc.vector.tensor_copy(slot_scales[:], token_scales[:].indirect(offsets[:]))
         gather_tokens(0)
-        weights(first_shared, 2)
-        weights(0, 2)
-        shared_pass(0)
+        for q in range(4):
+            nc.sync.dma_start(
+                token_scales[32 * q : 32 * q + 4 * LAST, :].bitcast(I32),
+                x_scales[:LAST, 4 * q : 4 * q + 4, :].bitcast(I32),
+            )
         spread_gate()
+        load_weights(sh, 2, sh)
+        load_weights(sh + 2, 2, sh)
+        for q in range(4):
+            nc.sync.dma_start(
+                token_scales[32 * q + 4 * LAST : 32 * q + 4 * PASSES, :].bitcast(I32),
+                x_scales[LAST, 4 * q : 4 * q + 4, :].bitcast(I32),
+            )
+        nc.vector.tensor_copy(slot_scales[:], token_scales[:].indirect(offsets[:]))
+        quantize_weights(sh, 4)
+        shared_pass(0)
+        load_weights(0, 2, 0)
         load_tokens(1)
         gather_tokens(1)
         shared_pass(1)
-        weights(2, 2)
-        weights(4, 2)
+        load_weights(2, 2, 0)
+        quantize_weights(0, 4)
+        load_weights(4, 2, 4)
         load_tokens(2)
         gather_tokens(2)
+        shared_pass(2)
         for q in range(4):
             nc.sync.dma_start(
                 slot_scales_last[32 * q : 32 * q + 4, :].bitcast(I32),
                 slot_scales[32 * q + 16 : 32 * q + 20, :].bitcast(I32),
             )
-        weights(6, 2)
-        weights(first_shared + 2, 2)
-        shared_pass(2)
+        load_weights(6, 2, 4)
+        quantize_weights(4, 4)
+        nc.sync.dma_start(bias[:], b)
+        load_weights(8, 2, 8)
         load_tokens(3)
         gather_tokens(3)
         shared_pass(3)
@@ -177,27 +203,33 @@ def tile_moe_shr_lin_bias_kernel(tc, x_words, x_scales, w, b, gate, offs, out):
                 token_scales_last[32 * q : 32 * q + 4, :].bitcast(I32),
                 x_scales[LAST, 4 * q : 4 * q + 4, :].bitcast(I32),
             )
-        weights(8, 2)
-        weights(10, 2)
+        load_weights(10, 2, 8)
+        quantize_weights(8, 4)
+        load_weights(12, 2, 12)
         load_tokens(4)
         gather_tokens(4)
-        weights(12, 2)
-        weights(14, 2)
-        weights(16, 2)
-        expert(0, 14)
-        expert(1, 16)
-        weights(first_shared + 4, 1)
+        load_weights(14, 2, 12)
+        quantize_weights(12, 4)
+        load_weights(16, 2, 16)
+        load_weights(18, 2, 16)
+        quantize_weights(16, 4)
+        experts(0, 2, 18)
+        load_weights(20, 2, 20)
+        load_weights(22, 2, 20)
+        quantize_weights(20, 4)
+        load_weights(24, 2, 24)
+        quantize_weights(24, 2)
+        experts(2, 1, 24)
+        load_weights(26, 2, 26)
+        quantize_weights(26, 2)
+        experts(3, 1, 26)
+        load_weights(28, 2, 28)
+        quantize_weights(28, 2)
+        load_weights(sh + 4, 1, sh + 4)
+        quantize_weights(sh + 4, 1)
         shared_pass(4)
-        weights(18, 2)
-        weights(20, 2)
-        expert(2, 20)
-        weights(22, 2)
-        weights(24, 2)
-        expert(3, 24)
-        weights(26, 2)
-        weights(28, 2)
-        expert(4, 26)
-        expert(5, 28)
+        experts(4, 1, 28)
+        experts(5, 1, sh + 4)
 
         for i in range(T // BANK):
             cols = slice(i * BANK, (i + 1) * BANK)

@@ -162,19 +162,13 @@ def tile_moe_shr_lin_bias_kernel(tc, x_words, x_scales, w, b, gate, offs, out):
         gather_tokens(0)
         for q in range(4):
             nc.sync.dma_start(
-                token_scales[32 * q : 32 * q + 4 * LAST, :].bitcast(I32),
-                x_scales[:LAST, 4 * q : 4 * q + 4, :].bitcast(I32),
-            )
-        spread_gate()
-        load_weights(sh, 2, sh)
-        load_weights(sh + 2, 2, sh)
-        for q in range(4):
-            nc.sync.dma_start(
-                token_scales[32 * q + 4 * LAST : 32 * q + 4 * PASSES, :].bitcast(I32),
-                x_scales[LAST, 4 * q : 4 * q + 4, :].bitcast(I32),
+                token_scales[32 * q : 32 * q + 4 * PASSES, :].bitcast(I32),
+                x_scales[:, 4 * q : 4 * q + 4, :].bitcast(I32),
             )
         nc.vector.tensor_copy(slot_scales[:], token_scales[:].indirect(offsets[:]))
-        quantize_weights(sh, 4)
+        spread_gate()
+        load_weights(sh, 2, sh)
+        quantize_weights(sh, 2)
         shared_pass(0)
         load_weights(0, 2, 0)
         load_tokens(1)
@@ -182,53 +176,48 @@ def tile_moe_shr_lin_bias_kernel(tc, x_words, x_scales, w, b, gate, offs, out):
         shared_pass(1)
         load_weights(2, 2, 0)
         quantize_weights(0, 4)
-        load_weights(4, 2, 4)
         load_tokens(2)
         gather_tokens(2)
-        shared_pass(2)
-        for q in range(4):
-            nc.sync.dma_start(
-                slot_scales_last[32 * q : 32 * q + 4, :].bitcast(I32),
-                slot_scales[32 * q + 16 : 32 * q + 20, :].bitcast(I32),
-            )
+        load_weights(4, 2, 4)
+        nc.sync.dma_start(slot_scales_last[: P - 16, :].bitcast(I32), slot_scales[16:, :].bitcast(I32))
         load_weights(6, 2, 4)
         quantize_weights(4, 4)
-        nc.sync.dma_start(bias[:], b)
-        load_weights(8, 2, 8)
         load_tokens(3)
         gather_tokens(3)
-        shared_pass(3)
-        for q in range(4):
-            nc.sync.dma_start(
-                token_scales_last[32 * q : 32 * q + 4, :].bitcast(I32),
-                x_scales[LAST, 4 * q : 4 * q + 4, :].bitcast(I32),
-            )
-        load_weights(10, 2, 8)
-        quantize_weights(8, 4)
-        load_weights(12, 2, 12)
+        nc.sync.dma_start(bias[:], b)
+        load_weights(8, 2, 8)
         load_tokens(4)
         gather_tokens(4)
+        load_weights(10, 2, 8)
+        quantize_weights(8, 4)
+        experts(0, 1, 10)
+        load_weights(12, 2, 12)
         load_weights(14, 2, 12)
         quantize_weights(12, 4)
+        experts(1, 1, 14)
+        nc.sync.dma_start(token_scales_last[: P - 16, :].bitcast(I32), token_scales[16:, :].bitcast(I32))
         load_weights(16, 2, 16)
         load_weights(18, 2, 16)
         quantize_weights(16, 4)
-        experts(0, 2, 18)
+        experts(2, 1, 18)
+        load_weights(sh + 2, 2, sh + 2)
+        quantize_weights(sh + 2, 2)
+        shared_pass(2)
+        shared_pass(3)
         load_weights(20, 2, 20)
+        experts(3, 1, 20)
         load_weights(22, 2, 20)
         quantize_weights(20, 4)
         load_weights(24, 2, 24)
         quantize_weights(24, 2)
-        experts(2, 1, 24)
         load_weights(26, 2, 26)
         quantize_weights(26, 2)
-        experts(3, 1, 26)
         load_weights(28, 2, 28)
         quantize_weights(28, 2)
+        experts(4, 1, 28)
         load_weights(sh + 4, 1, sh + 4)
         quantize_weights(sh + 4, 1)
         shared_pass(4)
-        experts(4, 1, 28)
         experts(5, 1, sh + 4)
 
         for i in range(T // BANK):

@@ -19,13 +19,21 @@ MULT = mybir.AluOpType.mult
 IDENTITY = mybir.ActivationFunctionType.Identity
 
 P = 128
+QUADRANT = 32
 PACK = 4
 K_PASS = P * PACK
 PASSES = K // K_PASS
-BANK = 512
 LAST = PASSES - 1
-GATE_ROW = SLOTS // P
+BANK = 512
+PER_COLUMN = 16
+SHARED = E * PASSES
+GATE_RUN = SLOTS // P
+PAIR = 2
+GROUP = 4
 HEAD = 2
+WIDE_PIECES = 24
+VECTOR_CAST = 20
+TOKENS_BEFORE = (0, 2, 4, 6, 7)
 
 
 def tile_moe_shr_lin_bias_kernel(tc, x_words, x_scales, w, b, gate, offs, out):
@@ -38,7 +46,7 @@ def tile_moe_shr_lin_bias_kernel(tc, x_words, x_scales, w, b, gate, offs, out):
         psum_shared = ctx.enter_context(tc.psum_pool(name="psum_shared", bufs=1))
         psum_ring = ctx.enter_context(tc.psum_pool(name="psum_ring", bufs=4))
 
-        offsets = keep.tile([P, SLOTS // 16], U16, name="offsets")
+        offsets = keep.tile([P, SLOTS // PER_COLUMN], U16, name="offsets")
         nc.sync.dma_start(offsets[:], offs)
 
         token_scales = keep.tile([P, T], U8, name="token_scales", align_bytes=64)
@@ -55,173 +63,142 @@ def tile_moe_shr_lin_bias_kernel(tc, x_words, x_scales, w, b, gate, offs, out):
         slot_words = [keep.tile([P, SLOTS], U32, name="slot_words%d" % o, align_bytes=64) for o in range(LAST)]
         slot_words_head = keep.tile([P, HEAD * C], U32, name="slot_words_head", align_bytes=64)
         slot_words_tail = keep.tile([P, (E - HEAD) * C], U32, name="slot_words_tail", align_bytes=64)
-
-        def load_tokens(o):
-            nc.sync.dma_start(token_words[o][:].bitcast(I32), x_words[o].rearrange("p t r -> p (t r)").bitcast(I32))
-
-        def gather_tokens(o):
-            if o < LAST:
-                nc.vector.tensor_copy(slot_words[o][:], token_words[o][:].indirect(offsets[:]))
-            else:
-                nc.vector.tensor_copy(slot_words_head[:], token_words[o][:].indirect(offsets[:, : 16 * HEAD]))
-                nc.vector.tensor_copy(slot_words_tail[:], token_words[o][:].indirect(offsets[:, 16 * HEAD :]))
-
+        bias = keep.tile([P, E + 1], F32, name="bias")
+        gate_all = keep.tile([P, SLOTS], F32, name="gate_all")
+        shared_sums = [psum_shared.tile([P, BANK], F32, name="shared_sums%d" % i) for i in range(T // BANK)]
+        interleaved = {}
         w_codes = {}
         w_scales = {}
 
-        grouped = {}
+        def slot_offsets(first_expert, end_expert):
+            return offsets[:, first_expert * C // PER_COLUMN : end_expert * C // PER_COLUMN]
+
+        def gather_token_pass(o):
+            nc.sync.dma_start(token_words[o][:].bitcast(I32), x_words[o].rearrange("p t r -> p (t r)").bitcast(I32))
+            if o < LAST:
+                nc.vector.tensor_copy(slot_words[o][:], token_words[o][:].indirect(offsets[:]))
+            else:
+                nc.vector.tensor_copy(slot_words_head[:], token_words[o][:].indirect(slot_offsets(0, HEAD)))
+                nc.vector.tensor_copy(slot_words_tail[:], token_words[o][:].indirect(slot_offsets(HEAD, E)))
+
+        def gather_scales():
+            for q in range(P // QUADRANT):
+                nc.sync.dma_start(
+                    token_scales[QUADRANT * q : QUADRANT * q + PACK * PASSES, :].bitcast(I32),
+                    x_scales[:, PACK * q : PACK * (q + 1), :].bitcast(I32),
+                )
+            nc.vector.tensor_copy(slot_scales[:], token_scales[:].indirect(offsets[:]))
+
+        def shift_last_plane(target, source):
+            nc.sync.dma_start(target[: P - PACK * LAST, :].bitcast(I32), source[PACK * LAST :, :].bitcast(I32))
+
+        def spread_gate():
+            gate_row = keep.tile([P, GATE_RUN], F32, name="gate_row")
+            nc.sync.dma_start(gate_row[:], gate[0].rearrange("(p m) -> p m", m=GATE_RUN))
+            identity = keep.tile([P, P], F32, name="identity")
+            make_identity(nc, identity[:])
+            by_run = gate_all[:].rearrange("q (p m) -> q p m", m=GATE_RUN)
+            per_bank = BANK // P
+            for m0 in range(0, GATE_RUN, per_bank):
+                bank = psum_ring.tile([P, per_bank, P], F32, name="bank")
+                for r in range(per_bank):
+                    nc.tensor.transpose(bank[:, r, :], gate_row[:, m0 + r : m0 + r + 1].to_broadcast([P, P]), identity[:])
+                nc.scalar.copy(by_run[:, :, m0 : m0 + per_bank], bank[:].rearrange("q r p -> q p r"))
 
         def load_weights(first, count, group):
-            raw = keep.tile([P, 2, PACK, N], F32, name="raw%d" % first, tag="raw%d" % first)
+            raw = keep.tile([P, PAIR, PACK, N], F32, name="raw%d" % first, tag="raw%d" % first)
             nc.sync.dma_start(
                 raw[:, :count],
                 w_rows[first * K_PASS : (first + count) * K_PASS, :].rearrange("(u p j) n -> p u j n", p=P, j=PACK),
             )
             if first == group:
-                grouped[group] = cast_pool.tile([P, 4, N, PACK], BF16, name="grouped", align_bytes=64)
-            nc.scalar.copy(
-                grouped[group][:, first - group : first - group + count].rearrange("p u (c i) j -> p u c j i", i=4),
-                raw[:, :count].rearrange("p u j (c i) -> p u c j i", i=4),
-            )
+                interleaved[group] = cast_pool.tile([P, GROUP, N, PACK], BF16, name="interleaved", align_bytes=64)
+            target = interleaved[group][:, first - group : first - group + count].rearrange("p u (c i) j -> p u c j i", i=4)
+            source = raw[:, :count].rearrange("p u j (c i) -> p u c j i", i=4)
+            if first == VECTOR_CAST:
+                nc.vector.tensor_copy(target, source)
+            else:
+                nc.scalar.copy(target, source)
 
         def quantize_weights(group, count):
             codes = keep.tile([P, count * N], U32, name="codes%d" % group, align_bytes=64)
             scales = keep.tile([P, count * N], U8, name="scales%d" % group, align_bytes=64)
-            nc.vector.quantize_mx(codes[:].bitcast(FP8X4), scales[:], grouped[group][:, :count].rearrange("p u n j -> p (u n j)"))
+            nc.vector.quantize_mx(
+                codes[:].bitcast(FP8X4), scales[:], interleaved[group][:, :count].rearrange("p u n j -> p (u n j)")
+            )
             for u in range(count):
                 w_codes[group + u] = codes[:, u * N : (u + 1) * N]
                 w_scales[group + u] = scales[:, u * N : (u + 1) * N]
 
-        shared = [psum_shared.tile([P, BANK], F32, name="shared%d" % i) for i in range(T // BANK)]
+        def multiply(sums, piece, words, plane):
+            o = piece % PASSES
+            nc.tensor.matmul_mx(
+                sums,
+                lhsT=w_codes[piece].bitcast(FP8X4),
+                lhsT_scale=w_scales[piece],
+                rhs=words.bitcast(FP8X4),
+                rhs_scale=plane,
+                start=(o == 0),
+                stop=(o == LAST),
+            )
 
         def shared_pass(o):
             for i in range(T // BANK):
                 cols = slice(i * BANK, (i + 1) * BANK)
-                plane = token_scales[4 * o :, cols] if o < LAST else token_scales_last[:, cols]
-                nc.tensor.matmul_mx(
-                    shared[i][:],
-                    lhsT=w_codes[E * PASSES + o].bitcast(FP8X4),
-                    lhsT_scale=w_scales[E * PASSES + o],
-                    rhs=token_words[o][:, cols].bitcast(FP8X4),
-                    rhs_scale=plane,
-                    start=(o == 0),
-                    stop=(o == LAST),
-                )
+                plane = token_scales[PACK * o :, cols] if o < LAST else token_scales_last[:, cols]
+                multiply(shared_sums[i][:], SHARED + o, token_words[o][:, cols], plane)
 
-        bias = keep.tile([P, E + 1], F32, name="bias")
-        gate_all = keep.tile([P, SLOTS], F32, name="gate_all")
-
-        def spread_gate():
-            gate_row = keep.tile([P, GATE_ROW], F32, name="gate_row")
-            nc.sync.dma_start(gate_row[:], gate[0].rearrange("(p m) -> p m", m=GATE_ROW))
-            identity = keep.tile([P, P], F32, name="identity")
-            make_identity(nc, identity[:])
-            by_column = gate_all[:].rearrange("q (p m) -> q p m", m=GATE_ROW)
-            for g in range(GATE_ROW // 4):
-                bank = psum_ring.tile([P, 4, P], F32, name="bank")
-                for r in range(4):
-                    m = 4 * g + r
-                    nc.tensor.transpose(bank[:, r, :], gate_row[:, m : m + 1].to_broadcast([P, P]), identity[:])
-                nc.scalar.copy(by_column[:, :, 4 * g : 4 * g + 4], bank[:].rearrange("q r p -> q p r"))
-
-        def expert(e, y):
+        def routed_expert(e, staging):
             slots = slice(e * C, (e + 1) * C)
-            bank = psum_ring.tile([P, 4, P], F32, name="bank")
-            acc = bank[:].rearrange("q r p -> q (r p)")[:, :C]
-            for o in range(PASSES):
-                if o < LAST:
-                    words, plane = slot_words[o][:, slots], slot_scales[4 * o :, slots]
-                elif e < HEAD:
-                    words, plane = slot_words_head[:, slots], slot_scales_last[:, slots]
-                else:
-                    words, plane = slot_words_tail[:, (e - HEAD) * C : (e - HEAD + 1) * C], slot_scales_last[:, slots]
-                nc.tensor.matmul_mx(
-                    acc,
-                    lhsT=w_codes[e * PASSES + o].bitcast(FP8X4),
-                    lhsT_scale=w_scales[e * PASSES + o],
-                    rhs=words.bitcast(FP8X4),
-                    rhs_scale=plane,
-                    start=(o == 0),
-                    stop=(o == LAST),
-                )
-            nc.scalar.activation(y, acc, IDENTITY, bias=bias[:, e : e + 1])
+            bank = psum_ring.tile([P, BANK // P, P], F32, name="bank")
+            sums = bank[:].rearrange("q r p -> q (r p)")[:, :C]
+            for o in range(LAST):
+                multiply(sums, e * PASSES + o, slot_words[o][:, slots], slot_scales[PACK * o :, slots])
+            if e < HEAD:
+                words = slot_words_head[:, slots]
+            else:
+                words = slot_words_tail[:, (e - HEAD) * C : (e - HEAD + 1) * C]
+            multiply(sums, e * PASSES + LAST, words, slot_scales_last[:, slots])
+            y = keep.tile([P, C], F32, name="y%d" % e, tag="raw%d" % staging)
+            nc.scalar.activation(y[:], sums, IDENTITY, bias=bias[:, e : e + 1])
+            nc.vector.tensor_tensor(routed[:].indirect(slot_offsets(e, e + 1)), y[:], gate_all[:, slots], MULT)
 
-        def experts(first, count, reuse):
-            y = keep.tile([P, count * C], F32, name="y%d" % first, tag="raw%d" % reuse)
-            for i in range(count):
-                expert(first + i, y[:, i * C : (i + 1) * C])
-            nc.vector.tensor_tensor(
-                routed[:].indirect(offsets[:, 16 * first : 16 * (first + count)]),
-                y[:],
-                gate_all[:, first * C : (first + count) * C],
-                MULT,
-            )
+        loads = [(SHARED + u, PAIR, SHARED, GROUP) for u in range(0, LAST, PAIR)]
+        loads = loads + [(u, PAIR, u - u % GROUP, GROUP) for u in range(0, WIDE_PIECES, PAIR)]
+        loads = loads + [(u, PAIR, u, PAIR) for u in range(WIDE_PIECES, SHARED, PAIR)]
+        loads = loads + [(SHARED + LAST, 1, SHARED + LAST, 1)]
 
-        sh = E * PASSES
-        load_tokens(0)
-        gather_tokens(0)
-        for q in range(4):
-            nc.sync.dma_start(
-                token_scales[32 * q : 32 * q + 4 * PASSES, :].bitcast(I32),
-                x_scales[:, 4 * q : 4 * q + 4, :].bitcast(I32),
-            )
-        nc.vector.tensor_copy(slot_scales[:], token_scales[:].indirect(offsets[:]))
-        spread_gate()
-        load_weights(sh, 2, sh)
-        quantize_weights(sh, 2)
-        shared_pass(0)
-        load_weights(0, 2, 0)
-        load_tokens(1)
-        gather_tokens(1)
-        shared_pass(1)
-        load_weights(2, 2, 0)
-        quantize_weights(0, 4)
-        load_tokens(2)
-        gather_tokens(2)
-        load_weights(4, 2, 4)
-        nc.sync.dma_start(slot_scales_last[: P - 16, :].bitcast(I32), slot_scales[16:, :].bitcast(I32))
-        load_weights(6, 2, 4)
-        quantize_weights(4, 4)
-        load_tokens(3)
-        gather_tokens(3)
-        nc.sync.dma_start(bias[:], b)
-        load_weights(8, 2, 8)
-        load_tokens(4)
-        gather_tokens(4)
-        load_weights(10, 2, 8)
-        quantize_weights(8, 4)
-        experts(0, 1, 10)
-        load_weights(12, 2, 12)
-        load_weights(14, 2, 12)
-        quantize_weights(12, 4)
-        experts(1, 1, 14)
-        nc.sync.dma_start(token_scales_last[: P - 16, :].bitcast(I32), token_scales[16:, :].bitcast(I32))
-        load_weights(16, 2, 16)
-        load_weights(18, 2, 16)
-        quantize_weights(16, 4)
-        experts(2, 1, 18)
-        load_weights(sh + 2, 2, sh + 2)
-        quantize_weights(sh + 2, 2)
-        shared_pass(2)
-        shared_pass(3)
-        load_weights(20, 2, 20)
-        experts(3, 1, 20)
-        load_weights(22, 2, 20)
-        quantize_weights(20, 4)
-        load_weights(24, 2, 24)
-        quantize_weights(24, 2)
-        load_weights(26, 2, 26)
-        quantize_weights(26, 2)
-        load_weights(28, 2, 28)
-        quantize_weights(28, 2)
-        experts(4, 1, 28)
-        load_weights(sh + 4, 1, sh + 4)
-        quantize_weights(sh + 4, 1)
-        shared_pass(4)
-        experts(5, 1, sh + 4)
+        staging_of = [((e + 2) * PASSES - 1) // PAIR * PAIR for e in range(E - 1)]
+        staging_of[0] = max(staging_of[0], loads[TOKENS_BEFORE[LAST]][0])
+        staging_of = staging_of + [staging_of[-1] - PAIR]
+
+        for j, (first, count, group, group_count) in enumerate(loads):
+            if j in TOKENS_BEFORE:
+                o = TOKENS_BEFORE.index(j)
+                gather_token_pass(o)
+                if 0 < o < LAST:
+                    shared_pass(o)
+                if o == LAST - 1:
+                    shift_last_plane(slot_scales_last, slot_scales)
+                    nc.sync.dma_start(bias[:], b)
+            load_weights(first, count, group)
+            if j == 0:
+                spread_gate()
+                gather_scales()
+            if j == len(loads) - 1:
+                shift_last_plane(token_scales_last, token_scales)
+            if first + count == group + group_count:
+                quantize_weights(group, group_count)
+                if group == SHARED:
+                    shared_pass(0)
+                if group == SHARED + LAST:
+                    shared_pass(LAST)
+                    routed_expert(E - 1, staging_of[E - 1])
+            if first in staging_of[: E - 1]:
+                routed_expert(staging_of.index(first), first)
 
         for i in range(T // BANK):
             cols = slice(i * BANK, (i + 1) * BANK)
             result = keep.tile([P, BANK], F32, name="result%d" % i)
-            nc.vector.scalar_tensor_tensor(result[:], shared[i][:], bias[:, E : E + 1], routed[:, cols], ADD, ADD)
+            nc.vector.scalar_tensor_tensor(result[:], shared_sums[i][:], bias[:, E : E + 1], routed[:, cols], ADD, ADD)
             nc.sync.dma_start(out[:, cols], result[:])

@@ -55,8 +55,6 @@ def tile_moe_shr_lin_bias_kernel(tc, x_words, x_scales, w, b, gate, offs, out):
         slot_scales_last = keep.tile([P, SLOTS], U8, name="slot_scales_last", align_bytes=64)
         routed = keep.tile([P, T], F32, name="routed")
         nc.vector.memset(token_scales[:].bitcast(I32), 0)
-        nc.vector.memset(token_scales_last[:].bitcast(I32), 0)
-        nc.vector.memset(slot_scales_last[:].bitcast(I32), 0)
         nc.vector.memset(routed[:], 0.0)
 
         token_words = [keep.tile([P, T], U32, name="token_words%d" % o, align_bytes=64) for o in range(PASSES)]
@@ -163,10 +161,10 @@ def tile_moe_shr_lin_bias_kernel(tc, x_words, x_scales, w, b, gate, offs, out):
             nc.scalar.activation(y[:], sums, IDENTITY, bias=bias[:, e : e + 1])
             nc.vector.tensor_tensor(routed[:].indirect(slot_offsets(e, e + 1)), y[:], gate_all[:, slots], MULT)
 
-        loads = [(SHARED + u, PAIR, SHARED, GROUP) for u in range(0, LAST, PAIR)]
+        loads = [(SHARED, PAIR, SHARED, PAIR), (SHARED + PAIR, 1, SHARED + PAIR, 1)]
         loads = loads + [(u, PAIR, u - u % GROUP, GROUP) for u in range(0, WIDE_PIECES, PAIR)]
         loads = loads + [(u, PAIR, u, PAIR) for u in range(WIDE_PIECES, SHARED, PAIR)]
-        loads = loads + [(SHARED + LAST, 1, SHARED + LAST, 1)]
+        loads = loads + [(SHARED + o, 1, SHARED + o, 1) for o in range(PAIR + 1, PASSES)]
 
         staging_of = [((e + 2) * PASSES - 1) // PAIR * PAIR for e in range(E - 1)]
         staging_of[0] = max(staging_of[0], loads[TOKENS_BEFORE[LAST]][0])
@@ -176,7 +174,7 @@ def tile_moe_shr_lin_bias_kernel(tc, x_words, x_scales, w, b, gate, offs, out):
             if j in TOKENS_BEFORE:
                 o = TOKENS_BEFORE.index(j)
                 gather_token_pass(o)
-                if 0 < o < LAST:
+                if 0 < o <= PAIR:
                     shared_pass(o)
                 if o == LAST - 1:
                     shift_last_plane(slot_scales_last, slot_scales)
@@ -191,14 +189,16 @@ def tile_moe_shr_lin_bias_kernel(tc, x_words, x_scales, w, b, gate, offs, out):
                 quantize_weights(group, group_count)
                 if group == SHARED:
                     shared_pass(0)
+                if group > SHARED + PAIR:
+                    shared_pass(group - SHARED)
                 if group == SHARED + LAST:
-                    shared_pass(LAST)
                     routed_expert(E - 1, staging_of[E - 1])
             if first in staging_of[: E - 1]:
                 routed_expert(staging_of.index(first), first)
 
-        for i in range(T // BANK):
-            cols = slice(i * BANK, (i + 1) * BANK)
-            result = keep.tile([P, BANK], F32, name="result%d" % i)
-            nc.vector.scalar_tensor_tensor(result[:], shared_sums[i][:], bias[:, E : E + 1], routed[:, cols], ADD, ADD)
-            nc.sync.dma_start(out[:, cols], result[:])
+        starts = list(range(0, T, BANK)) + [T - BANK // 2, T]
+        for start, end in zip(starts, starts[1:]):
+            sums = shared_sums[start // BANK][:, start % BANK : start % BANK + end - start]
+            result = keep.tile([P, end - start], F32, name="result%d" % start)
+            nc.vector.scalar_tensor_tensor(result[:], sums, bias[:, E : E + 1], routed[:, start:end], ADD, ADD)
+            nc.sync.dma_start(out[:, start:end], result[:])

@@ -16,7 +16,7 @@ U8 = mybir.dt.uint8
 FP8X4 = mybir.dt.float8_e4m3fn_x4
 ADD = mybir.AluOpType.add
 MULT = mybir.AluOpType.mult
-IDENTITY = mybir.ActivationFunctionType.Identity
+COPY = mybir.ActivationFunctionType.Copy
 
 P = 128
 QUADRANT = 32
@@ -28,12 +28,13 @@ BANK = 512
 PER_COLUMN = 16
 SHARED = E * PASSES
 GATE_RUN = SLOTS // P
-PAIR = 2
-GROUP = 4
-HEAD = 2
-WIDE_PIECES = 24
-VECTOR_CAST = 20
-TOKENS_BEFORE = (0, 2, 4, 6, 7)
+EARLY_EXPERTS = 3
+EARLY_LOADS = (
+    ((SHARED, 2), (SHARED + 2, 2), (0, 2)),
+    ((2, 4),),
+    ((6, 4),),
+    ((10, 3), (13, 3)),
+)
 
 
 def tile_moe_shr_lin_bias_kernel(tc, x_words, x_scales, w, b, gate, offs, out):
@@ -42,7 +43,7 @@ def tile_moe_shr_lin_bias_kernel(tc, x_words, x_scales, w, b, gate, offs, out):
 
     with ExitStack() as ctx:
         keep = ctx.enter_context(tc.tile_pool(name="keep", bufs=1))
-        cast_pool = ctx.enter_context(tc.tile_pool(name="cast", bufs=5))
+        last_pool = ctx.enter_context(tc.tile_pool(name="last", bufs=3))
         psum_shared = ctx.enter_context(tc.psum_pool(name="psum_shared", bufs=1))
         psum_ring = ctx.enter_context(tc.psum_pool(name="psum_ring", bufs=4))
 
@@ -59,8 +60,7 @@ def tile_moe_shr_lin_bias_kernel(tc, x_words, x_scales, w, b, gate, offs, out):
 
         token_words = [keep.tile([P, T], U32, name="token_words%d" % o, align_bytes=64) for o in range(PASSES)]
         slot_words = [keep.tile([P, SLOTS], U32, name="slot_words%d" % o, align_bytes=64) for o in range(LAST)]
-        slot_words_head = keep.tile([P, HEAD * C], U32, name="slot_words_head", align_bytes=64)
-        slot_words_tail = keep.tile([P, (E - HEAD) * C], U32, name="slot_words_tail", align_bytes=64)
+        slot_words_last = {}
         bias = keep.tile([P, E + 1], F32, name="bias")
         gate_all = keep.tile([P, SLOTS], F32, name="gate_all")
         shared_sums = [psum_shared.tile([P, BANK], F32, name="shared_sums%d" % i) for i in range(T // BANK)]
@@ -68,27 +68,37 @@ def tile_moe_shr_lin_bias_kernel(tc, x_words, x_scales, w, b, gate, offs, out):
         w_codes = {}
         w_scales = {}
 
-        def slot_offsets(first_expert, end_expert):
-            return offsets[:, first_expert * C // PER_COLUMN : end_expert * C // PER_COLUMN]
+        def slot_offsets(e):
+            return offsets[:, e * C // PER_COLUMN : (e + 1) * C // PER_COLUMN]
 
-        def gather_token_pass(o):
+        def load_tokens(o):
             nc.sync.dma_start(token_words[o][:].bitcast(I32), x_words[o].rearrange("p t r -> p (t r)").bitcast(I32))
-            if o < LAST:
-                nc.vector.tensor_copy(slot_words[o][:], token_words[o][:].indirect(offsets[:]))
-            else:
-                nc.vector.tensor_copy(slot_words_head[:], token_words[o][:].indirect(slot_offsets(0, HEAD)))
-                nc.vector.tensor_copy(slot_words_tail[:], token_words[o][:].indirect(slot_offsets(HEAD, E)))
 
-        def gather_scales():
+        def load_scales():
             for q in range(P // QUADRANT):
                 nc.sync.dma_start(
-                    token_scales[QUADRANT * q : QUADRANT * q + PACK * PASSES, :].bitcast(I32),
-                    x_scales[:, PACK * q : PACK * (q + 1), :].bitcast(I32),
+                    token_scales[QUADRANT * q : QUADRANT * q + PACK * LAST, :].bitcast(I32),
+                    x_scales[:LAST, PACK * q : PACK * (q + 1), :].bitcast(I32),
                 )
+            nc.sync.dma_start(token_scales[PACK * LAST : QUADRANT, :].bitcast(I32), x_scales[LAST].bitcast(I32))
+
+        def gather_scales():
             nc.vector.tensor_copy(slot_scales[:], token_scales[:].indirect(offsets[:]))
 
-        def shift_last_plane(target, source):
-            nc.sync.dma_start(target[: P - PACK * LAST, :].bitcast(I32), source[PACK * LAST :, :].bitcast(I32))
+        def load_last_scales():
+            for q in range(P // QUADRANT):
+                nc.sync.dma_start(
+                    token_scales_last[QUADRANT * q : QUADRANT * q + PACK, :].bitcast(I32),
+                    x_scales[LAST, PACK * q : PACK * (q + 1), :].bitcast(I32),
+                )
+
+        def shift_last_plane():
+            for q in range(P // QUADRANT):
+                row = PACK * (LAST + q)
+                nc.sync.dma_start(
+                    slot_scales_last[QUADRANT * q : QUADRANT * q + PACK, :].bitcast(I32),
+                    slot_scales[row : row + PACK, :].bitcast(I32),
+                )
 
         def spread_gate():
             gate_row = keep.tile([P, GATE_RUN], F32, name="gate_row")
@@ -101,29 +111,26 @@ def tile_moe_shr_lin_bias_kernel(tc, x_words, x_scales, w, b, gate, offs, out):
                 bank = psum_ring.tile([P, per_bank, P], F32, name="bank")
                 for r in range(per_bank):
                     nc.tensor.transpose(bank[:, r, :], gate_row[:, m0 + r : m0 + r + 1].to_broadcast([P, P]), identity[:])
-                nc.scalar.copy(by_run[:, :, m0 : m0 + per_bank], bank[:].rearrange("q r p -> q p r"))
+                nc.scalar.activation(by_run[:, :, m0 : m0 + per_bank], bank[:].rearrange("q r p -> q p r"), COPY)
 
-        def load_weights(first, count, group):
-            raw = keep.tile([P, PAIR, PACK, N], F32, name="raw%d" % first, tag="raw%d" % first)
+        def staging(first):
+            return "raw%d" % first
+
+        def load_weights(first, count, group, group_count, cast):
+            raw = keep.tile([P, count, PACK, N], F32, name=staging(first), tag=staging(first), align_bytes=64)
             nc.sync.dma_start(
-                raw[:, :count],
+                raw[:],
                 w_rows[first * K_PASS : (first + count) * K_PASS, :].rearrange("(u p j) n -> p u j n", p=P, j=PACK),
             )
             if first == group:
-                interleaved[group] = cast_pool.tile([P, GROUP, N, PACK], BF16, name="interleaved", align_bytes=64)
+                interleaved[group] = keep.tile([P, group_count, N, PACK], BF16, name="interleaved%d" % group, align_bytes=64)
             target = interleaved[group][:, first - group : first - group + count].rearrange("p u (c i) j -> p u c j i", i=4)
-            source = raw[:, :count].rearrange("p u j (c i) -> p u c j i", i=4)
-            if first == VECTOR_CAST:
-                nc.vector.tensor_copy(target, source)
-            else:
-                nc.scalar.copy(target, source)
+            cast(target, raw[:].rearrange("p u j (c i) -> p u c j i", i=4))
 
-        def quantize_weights(group, count):
-            codes = keep.tile([P, count * N], U32, name="codes%d" % group, align_bytes=64)
+        def quantize_weights(group, count, tag):
+            codes = keep.tile([P, count * N], U32, name="codes%d" % group, tag=tag, align_bytes=64)
             scales = keep.tile([P, count * N], U8, name="scales%d" % group, align_bytes=64)
-            nc.vector.quantize_mx(
-                codes[:].bitcast(FP8X4), scales[:], interleaved[group][:, :count].rearrange("p u n j -> p (u n j)")
-            )
+            nc.vector.quantize_mx(codes[:].bitcast(FP8X4), scales[:], interleaved[group][:].rearrange("p u n j -> p (u n j)"))
             for u in range(count):
                 w_codes[group + u] = codes[:, u * N : (u + 1) * N]
                 w_scales[group + u] = scales[:, u * N : (u + 1) * N]
@@ -146,55 +153,62 @@ def tile_moe_shr_lin_bias_kernel(tc, x_words, x_scales, w, b, gate, offs, out):
                 plane = token_scales[PACK * o :, cols] if o < LAST else token_scales_last[:, cols]
                 multiply(shared_sums[i][:], SHARED + o, token_words[o][:, cols], plane)
 
-        def routed_expert(e, staging):
+        def gather_last(e):
+            slot_words_last[e] = last_pool.tile([P, C], U32, name="slot_words_last", align_bytes=64)
+            nc.vector.tensor_copy(slot_words_last[e][:], token_words[LAST][:].indirect(slot_offsets(e)))
+
+        def routed_expert(e, tag):
             slots = slice(e * C, (e + 1) * C)
             bank = psum_ring.tile([P, BANK // P, P], F32, name="bank")
             sums = bank[:].rearrange("q r p -> q (r p)")[:, :C]
             for o in range(LAST):
                 multiply(sums, e * PASSES + o, slot_words[o][:, slots], slot_scales[PACK * o :, slots])
-            if e < HEAD:
-                words = slot_words_head[:, slots]
-            else:
-                words = slot_words_tail[:, (e - HEAD) * C : (e - HEAD + 1) * C]
-            multiply(sums, e * PASSES + LAST, words, slot_scales_last[:, slots])
-            y = keep.tile([P, C], F32, name="y%d" % e, tag="raw%d" % staging)
-            nc.scalar.activation(y[:], sums, IDENTITY, bias=bias[:, e : e + 1])
-            nc.vector.tensor_tensor(routed[:].indirect(slot_offsets(e, e + 1)), y[:], gate_all[:, slots], MULT)
+            multiply(sums, e * PASSES + LAST, slot_words_last[e][:], slot_scales_last[:, slots])
+            y = keep.tile([P, C], F32, name="y%d" % e, tag=tag, align_bytes=64)
+            nc.vector.scalar_tensor_tensor(y[:], sums, bias[:, e : e + 1], gate_all[:, slots], ADD, MULT)
+            nc.scalar.activation(routed[:].indirect(slot_offsets(e)), y[:], COPY)
 
-        loads = [(SHARED, PAIR, SHARED, PAIR), (SHARED + PAIR, 1, SHARED + PAIR, 1)]
-        loads = loads + [(u, PAIR, u - u % GROUP, GROUP) for u in range(0, WIDE_PIECES, PAIR)]
-        loads = loads + [(u, PAIR, u, PAIR) for u in range(WIDE_PIECES, SHARED, PAIR)]
-        loads = loads + [(SHARED + o, 1, SHARED + o, 1) for o in range(PAIR + 1, PASSES)]
-
-        staging_of = [((e + 2) * PASSES - 1) // PAIR * PAIR for e in range(E - 1)]
-        staging_of[0] = max(staging_of[0], loads[TOKENS_BEFORE[LAST]][0])
-        staging_of = staging_of + [staging_of[-1] - PAIR]
-
-        for j, (first, count, group, group_count) in enumerate(loads):
-            if j in TOKENS_BEFORE:
-                o = TOKENS_BEFORE.index(j)
-                gather_token_pass(o)
-                if 0 < o <= PAIR:
-                    shared_pass(o)
-                if o == LAST - 1:
-                    shift_last_plane(slot_scales_last, slot_scales)
-                    nc.sync.dma_start(bias[:], b)
-            load_weights(first, count, group)
-            if j == 0:
-                spread_gate()
+        spread_gate()
+        for o in range(LAST):
+            load_tokens(o)
+            nc.vector.tensor_copy(slot_words[o][:], token_words[o][:].indirect(offsets[:]))
+            if o == 0:
+                load_scales()
                 gather_scales()
-            if j == len(loads) - 1:
-                shift_last_plane(token_scales_last, token_scales)
-            if first + count == group + group_count:
-                quantize_weights(group, group_count)
-                if group == SHARED:
-                    shared_pass(0)
-                if group > SHARED + PAIR:
-                    shared_pass(group - SHARED)
-                if group == SHARED + LAST:
-                    routed_expert(E - 1, staging_of[E - 1])
-            if first in staging_of[: E - 1]:
-                routed_expert(staging_of.index(first), first)
+            if o == 1:
+                nc.sync.dma_start(bias[:], b)
+            if o == LAST - 1:
+                shift_last_plane()
+            for first, count in EARLY_LOADS[o]:
+                load_weights(first, count, first, count, nc.scalar.copy)
+                quantize_weights(first, count, "codes%d" % first)
+            if o > 0:
+                shared_pass(o - 1)
+        shared_pass(LAST - 1)
+
+        load_tokens(LAST)
+        for e in range(EARLY_EXPERTS):
+            gather_last(e)
+        for e in range(EARLY_EXPERTS):
+            routed_expert(e, "y%d" % e)
+            gather_last(e + EARLY_EXPERTS)
+
+        for e in range(EARLY_EXPERTS, E):
+            first = e * PASSES
+            group = first + 1 if e == EARLY_EXPERTS else first
+            if group == first:
+                load_weights(first, 1, group, 3, nc.scalar.copy)
+            load_weights(first + 1, 2, group, first + 3 - group, nc.vector.tensor_copy)
+            if e > EARLY_EXPERTS:
+                routed_expert(e - 1, staging(first + 1))
+            load_weights(first + 3, 2, first + 3, 2, nc.vector.tensor_copy)
+            quantize_weights(group, first + 3 - group, staging(first + 3))
+            quantize_weights(first + 3, 2, "codes%d" % (first + 3))
+        load_last_scales()
+        load_weights(SHARED + LAST, 1, SHARED + LAST, 1, nc.vector.tensor_copy)
+        routed_expert(E - 1, staging(SHARED + LAST))
+        quantize_weights(SHARED + LAST, 1, "codes%d" % (SHARED + LAST))
+        shared_pass(LAST)
 
         starts = list(range(0, T, BANK)) + [T - BANK // 2, T]
         for start, end in zip(starts, starts[1:]):

@@ -28,13 +28,11 @@ BANK = 512
 PER_COLUMN = 16
 SHARED = E * PASSES
 GATE_RUN = SLOTS // P
-EARLY_EXPERTS = 3
-EARLY_LOADS = (
-    ((SHARED, 2), (SHARED + 2, 2), (0, 2)),
-    ((2, 4),),
-    ((6, 4),),
-    ((10, 3), (13, 3)),
-)
+HEAD = 2
+EARLY_SHARED = 2
+SCALAR_EXPERTS = 3
+FIRST_LOAD = 2
+PAIR = 2
 
 
 def tile_moe_shr_lin_bias_kernel(tc, x_words, x_scales, w, b, gate, offs, out):
@@ -43,12 +41,10 @@ def tile_moe_shr_lin_bias_kernel(tc, x_words, x_scales, w, b, gate, offs, out):
 
     with ExitStack() as ctx:
         keep = ctx.enter_context(tc.tile_pool(name="keep", bufs=1))
-        last_pool = ctx.enter_context(tc.tile_pool(name="last", bufs=3))
         psum_shared = ctx.enter_context(tc.psum_pool(name="psum_shared", bufs=1))
         psum_ring = ctx.enter_context(tc.psum_pool(name="psum_ring", bufs=4))
 
         offsets = keep.tile([P, SLOTS // PER_COLUMN], U16, name="offsets")
-        nc.sync.dma_start(offsets[:], offs)
 
         token_scales = keep.tile([P, T], U8, name="token_scales", align_bytes=64)
         token_scales_last = keep.tile([P, T], U8, name="token_scales_last", align_bytes=64)
@@ -60,7 +56,8 @@ def tile_moe_shr_lin_bias_kernel(tc, x_words, x_scales, w, b, gate, offs, out):
 
         token_words = [keep.tile([P, T], U32, name="token_words%d" % o, align_bytes=64) for o in range(PASSES)]
         slot_words = [keep.tile([P, SLOTS], U32, name="slot_words%d" % o, align_bytes=64) for o in range(LAST)]
-        slot_words_last = {}
+        slot_words_head = keep.tile([P, HEAD * C], U32, name="slot_words_head", align_bytes=64)
+        slot_words_tail = keep.tile([P, (E - HEAD) * C], U32, name="slot_words_tail", align_bytes=64)
         bias = keep.tile([P, E + 1], F32, name="bias")
         gate_all = keep.tile([P, SLOTS], F32, name="gate_all")
         shared_sums = [psum_shared.tile([P, BANK], F32, name="shared_sums%d" % i) for i in range(T // BANK)]
@@ -68,37 +65,29 @@ def tile_moe_shr_lin_bias_kernel(tc, x_words, x_scales, w, b, gate, offs, out):
         w_codes = {}
         w_scales = {}
 
-        def slot_offsets(e):
-            return offsets[:, e * C // PER_COLUMN : (e + 1) * C // PER_COLUMN]
+        def slot_offsets(first_expert, end_expert):
+            return offsets[:, first_expert * C // PER_COLUMN : end_expert * C // PER_COLUMN]
 
-        def load_tokens(o):
+        def gather_token_pass(o):
             nc.sync.dma_start(token_words[o][:].bitcast(I32), x_words[o].rearrange("p t r -> p (t r)").bitcast(I32))
-
-        def load_scales():
-            for q in range(P // QUADRANT):
-                nc.sync.dma_start(
-                    token_scales[QUADRANT * q : QUADRANT * q + PACK * LAST, :].bitcast(I32),
-                    x_scales[:LAST, PACK * q : PACK * (q + 1), :].bitcast(I32),
-                )
-            nc.sync.dma_start(token_scales[PACK * LAST : QUADRANT, :].bitcast(I32), x_scales[LAST].bitcast(I32))
+            if o == 0:
+                nc.sync.dma_start(offsets[:], offs)
+            if o < LAST:
+                nc.vector.tensor_copy(slot_words[o][:], token_words[o][:].indirect(offsets[:]))
+            else:
+                nc.vector.tensor_copy(slot_words_head[:], token_words[o][:].indirect(slot_offsets(0, HEAD)))
+                nc.vector.tensor_copy(slot_words_tail[:], token_words[o][:].indirect(slot_offsets(HEAD, E)))
 
         def gather_scales():
+            for q in range(P // QUADRANT):
+                nc.sync.dma_start(
+                    token_scales[QUADRANT * q : QUADRANT * q + PACK * PASSES, :].bitcast(I32),
+                    x_scales[:, PACK * q : PACK * (q + 1), :].bitcast(I32),
+                )
             nc.vector.tensor_copy(slot_scales[:], token_scales[:].indirect(offsets[:]))
 
-        def load_last_scales():
-            for q in range(P // QUADRANT):
-                nc.sync.dma_start(
-                    token_scales_last[QUADRANT * q : QUADRANT * q + PACK, :].bitcast(I32),
-                    x_scales[LAST, PACK * q : PACK * (q + 1), :].bitcast(I32),
-                )
-
-        def shift_last_plane():
-            for q in range(P // QUADRANT):
-                row = PACK * (LAST + q)
-                nc.sync.dma_start(
-                    slot_scales_last[QUADRANT * q : QUADRANT * q + PACK, :].bitcast(I32),
-                    slot_scales[row : row + PACK, :].bitcast(I32),
-                )
+        def shift_last_plane(target, source):
+            nc.sync.dma_start(target[: P - PACK * LAST, :].bitcast(I32), source[PACK * LAST :, :].bitcast(I32))
 
         def spread_gate():
             gate_row = keep.tile([P, GATE_RUN], F32, name="gate_row")
@@ -113,27 +102,27 @@ def tile_moe_shr_lin_bias_kernel(tc, x_words, x_scales, w, b, gate, offs, out):
                     nc.tensor.transpose(bank[:, r, :], gate_row[:, m0 + r : m0 + r + 1].to_broadcast([P, P]), identity[:])
                 nc.scalar.activation(by_run[:, :, m0 : m0 + per_bank], bank[:].rearrange("q r p -> q p r"), COPY)
 
-        def staging(first):
-            return "raw%d" % first
-
-        def load_weights(first, count, group, group_count, cast):
-            raw = keep.tile([P, count, PACK, N], F32, name=staging(first), tag=staging(first), align_bytes=64)
+        def load_weights(first, count, group, group_count, cast, tag=None):
+            raw = keep.tile([P, count, PACK, N], F32, name="raw%d" % first, tag="raw%d" % first, align_bytes=64)
             nc.sync.dma_start(
                 raw[:],
                 w_rows[first * K_PASS : (first + count) * K_PASS, :].rearrange("(u p j) n -> p u j n", p=P, j=PACK),
             )
             if first == group:
-                interleaved[group] = keep.tile([P, group_count, N, PACK], BF16, name="interleaved%d" % group, align_bytes=64)
-            target = interleaved[group][:, first - group : first - group + count].rearrange("p u (c i) j -> p u c j i", i=4)
-            cast(target, raw[:].rearrange("p u j (c i) -> p u c j i", i=4))
+                name = "interleaved%d" % group
+                interleaved[group] = keep.tile([P, group_count, N, PACK], BF16, name=name, tag=tag or name, align_bytes=64)
+            cast(
+                interleaved[group][:, first - group : first - group + count].rearrange("p u (c i) j -> p u c j i", i=4),
+                raw[:].rearrange("p u j (c i) -> p u c j i", i=4),
+            )
 
-        def quantize_weights(group, count, tag):
-            codes = keep.tile([P, count * N], U32, name="codes%d" % group, tag=tag, align_bytes=64)
-            scales = keep.tile([P, count * N], U8, name="scales%d" % group, align_bytes=64)
-            nc.vector.quantize_mx(codes[:].bitcast(FP8X4), scales[:], interleaved[group][:].rearrange("p u n j -> p (u n j)"))
+        def quantize_weights(first, count, tag):
+            codes = keep.tile([P, count * N], U32, name="codes%d" % first, tag=tag, align_bytes=64)
+            scales = keep.tile([P, count * N], U8, name="scales%d" % first, align_bytes=64)
+            nc.vector.quantize_mx(codes[:].bitcast(FP8X4), scales[:], interleaved[first][:].rearrange("p u n j -> p (u n j)"))
             for u in range(count):
-                w_codes[group + u] = codes[:, u * N : (u + 1) * N]
-                w_scales[group + u] = scales[:, u * N : (u + 1) * N]
+                w_codes[first + u] = codes[:, u * N : (u + 1) * N]
+                w_scales[first + u] = scales[:, u * N : (u + 1) * N]
 
         def multiply(sums, piece, words, plane):
             o = piece % PASSES
@@ -147,68 +136,69 @@ def tile_moe_shr_lin_bias_kernel(tc, x_words, x_scales, w, b, gate, offs, out):
                 stop=(o == LAST),
             )
 
-        def shared_pass(o):
+        def shared_passes(passes):
             for i in range(T // BANK):
                 cols = slice(i * BANK, (i + 1) * BANK)
-                plane = token_scales[PACK * o :, cols] if o < LAST else token_scales_last[:, cols]
-                multiply(shared_sums[i][:], SHARED + o, token_words[o][:, cols], plane)
+                for o in passes:
+                    plane = token_scales[PACK * o :, cols] if o < LAST else token_scales_last[:, cols]
+                    multiply(shared_sums[i][:], SHARED + o, token_words[o][:, cols], plane)
 
-        def gather_last(e):
-            slot_words_last[e] = last_pool.tile([P, C], U32, name="slot_words_last", align_bytes=64)
-            nc.vector.tensor_copy(slot_words_last[e][:], token_words[LAST][:].indirect(slot_offsets(e)))
-
-        def routed_expert(e, tag):
+        def routed_expert(e, staging):
             slots = slice(e * C, (e + 1) * C)
             bank = psum_ring.tile([P, BANK // P, P], F32, name="bank")
             sums = bank[:].rearrange("q r p -> q (r p)")[:, :C]
             for o in range(LAST):
                 multiply(sums, e * PASSES + o, slot_words[o][:, slots], slot_scales[PACK * o :, slots])
-            multiply(sums, e * PASSES + LAST, slot_words_last[e][:], slot_scales_last[:, slots])
-            y = keep.tile([P, C], F32, name="y%d" % e, tag=tag, align_bytes=64)
+            if e < HEAD:
+                words = slot_words_head[:, slots]
+            else:
+                words = slot_words_tail[:, (e - HEAD) * C : (e - HEAD + 1) * C]
+            multiply(sums, e * PASSES + LAST, words, slot_scales_last[:, slots])
+            y = keep.tile([P, C], F32, name="y%d" % e, tag="raw%d" % staging, align_bytes=64)
             nc.vector.scalar_tensor_tensor(y[:], sums, bias[:, e : e + 1], gate_all[:, slots], ADD, MULT)
-            nc.scalar.activation(routed[:].indirect(slot_offsets(e)), y[:], COPY)
+            nc.scalar.activation(routed[:].indirect(slot_offsets(e, e + 1)), y[:], COPY)
 
+        def load_and_quantize(first, count, cast, leaving=None):
+            load_weights(first, count, first, count, cast)
+            if leaving is not None:
+                routed_expert(leaving, first)
+            quantize_weights(first, count, "codes%d" % first)
+
+        gather_token_pass(0)
         spread_gate()
-        for o in range(LAST):
-            load_tokens(o)
-            nc.vector.tensor_copy(slot_words[o][:], token_words[o][:].indirect(offsets[:]))
-            if o == 0:
-                load_scales()
-                gather_scales()
-            if o == 1:
-                nc.sync.dma_start(bias[:], b)
-            if o == LAST - 1:
-                shift_last_plane()
-            for first, count in EARLY_LOADS[o]:
-                load_weights(first, count, first, count, nc.scalar.copy)
-                quantize_weights(first, count, "codes%d" % first)
-            if o > 0:
-                shared_pass(o - 1)
-        shared_pass(LAST - 1)
+        nc.sync.dma_start(bias[:], b)
+        gather_scales()
+        load_and_quantize(SHARED, EARLY_SHARED, nc.scalar.copy)
+        shared_passes([0])
 
-        load_tokens(LAST)
-        for e in range(EARLY_EXPERTS):
-            gather_last(e)
-        for e in range(EARLY_EXPERTS):
-            routed_expert(e, "y%d" % e)
-            gather_last(e + EARLY_EXPERTS)
+        early = []
+        for e in range(SCALAR_EXPERTS):
+            early = early + [(e * PASSES, FIRST_LOAD), (e * PASSES + FIRST_LOAD, PASSES - FIRST_LOAD)]
+        for j, (first, count) in enumerate(early):
+            if 0 < j <= LAST:
+                gather_token_pass(j)
+                if j < EARLY_SHARED:
+                    shared_passes([j])
+                if j == LAST - 1:
+                    shift_last_plane(slot_scales_last, slot_scales)
+            load_and_quantize(first, count, nc.scalar.copy, j - LAST if j >= LAST else None)
 
-        for e in range(EARLY_EXPERTS, E):
+        for e in range(SCALAR_EXPERTS, E):
             first = e * PASSES
-            group = first + 1 if e == EARLY_EXPERTS else first
-            if group == first:
-                load_weights(first, 1, group, 3, nc.scalar.copy)
-            load_weights(first + 1, 2, group, first + 3 - group, nc.vector.tensor_copy)
-            if e > EARLY_EXPERTS:
-                routed_expert(e - 1, staging(first + 1))
-            load_weights(first + 3, 2, first + 3, 2, nc.vector.tensor_copy)
-            quantize_weights(group, first + 3 - group, staging(first + 3))
-            quantize_weights(first + 3, 2, "codes%d" % (first + 3))
-        load_last_scales()
-        load_weights(SHARED + LAST, 1, SHARED + LAST, 1, nc.vector.tensor_copy)
-        routed_expert(E - 1, staging(SHARED + LAST))
-        quantize_weights(SHARED + LAST, 1, "codes%d" % (SHARED + LAST))
-        shared_pass(LAST)
+            load_weights(first, 1, first, 1 + PAIR, nc.scalar.copy)
+            load_weights(first + 1, PAIR, first, 1 + PAIR, nc.vector.tensor_copy)
+            routed_expert(e - 1, first + 1)
+            load_weights(first + 1 + PAIR, PAIR, first + 1 + PAIR, PAIR, nc.vector.tensor_copy)
+            quantize_weights(first, 1 + PAIR, "raw%d" % (first + 1 + PAIR))
+            quantize_weights(first + 1 + PAIR, PAIR, "codes%d" % (first + 1 + PAIR))
+
+        late = SHARED + EARLY_SHARED
+        load_and_quantize(late, PASSES - EARLY_SHARED - PAIR, nc.vector.tensor_copy, E - 1)
+        last_pair = SHARED + PASSES - PAIR
+        load_weights(last_pair, PAIR, last_pair, PAIR, nc.vector.tensor_copy, "interleaved%d" % late)
+        quantize_weights(last_pair, PAIR, "codes%d" % last_pair)
+        shift_last_plane(token_scales_last, token_scales)
+        shared_passes(range(EARLY_SHARED, PASSES))
 
         starts = list(range(0, T, BANK)) + [T - BANK // 2, T]
         for start, end in zip(starts, starts[1:]):

@@ -28,11 +28,10 @@ BANK = 512
 PER_COLUMN = 16
 SHARED = E * PASSES
 GATE_RUN = SLOTS // P
-HEAD = 2
-EARLY_SHARED = 2
-SCALAR_EXPERTS = 3
 FIRST_LOAD = 2
-PAIR = 2
+EARLY_EXPERTS = E // 2
+EARLY_SHARED = 2
+HOSTS = (2, 4)
 
 
 def tile_moe_shr_lin_bias_kernel(tc, x_words, x_scales, w, b, gate, offs, out):
@@ -55,28 +54,25 @@ def tile_moe_shr_lin_bias_kernel(tc, x_words, x_scales, w, b, gate, offs, out):
         nc.vector.memset(routed[:], 0.0)
 
         token_words = [keep.tile([P, T], U32, name="token_words%d" % o, align_bytes=64) for o in range(PASSES)]
-        slot_words = [keep.tile([P, SLOTS], U32, name="slot_words%d" % o, align_bytes=64) for o in range(LAST)]
-        slot_words_head = keep.tile([P, HEAD * C], U32, name="slot_words_head", align_bytes=64)
-        slot_words_tail = keep.tile([P, (E - HEAD) * C], U32, name="slot_words_tail", align_bytes=64)
+        slot_words = {}
         bias = keep.tile([P, E + 1], F32, name="bias")
         gate_all = keep.tile([P, SLOTS], F32, name="gate_all")
         shared_sums = [psum_shared.tile([P, BANK], F32, name="shared_sums%d" % i) for i in range(T // BANK)]
-        interleaved = {}
         w_codes = {}
         w_scales = {}
 
         def slot_offsets(first_expert, end_expert):
             return offsets[:, first_expert * C // PER_COLUMN : end_expert * C // PER_COLUMN]
 
-        def gather_token_pass(o):
+        def load_tokens(o):
             nc.sync.dma_start(token_words[o][:].bitcast(I32), x_words[o].rearrange("p t r -> p (t r)").bitcast(I32))
-            if o == 0:
-                nc.sync.dma_start(offsets[:], offs)
-            if o < LAST:
-                nc.vector.tensor_copy(slot_words[o][:], token_words[o][:].indirect(offsets[:]))
-            else:
-                nc.vector.tensor_copy(slot_words_head[:], token_words[o][:].indirect(slot_offsets(0, HEAD)))
-                nc.vector.tensor_copy(slot_words_tail[:], token_words[o][:].indirect(slot_offsets(HEAD, E)))
+
+        def gather_words(o, first_expert, end_expert, tag):
+            shape = [P, (end_expert - first_expert) * C]
+            words = keep.tile(shape, U32, name="words%d_%d" % (o, first_expert), tag=tag, align_bytes=64)
+            nc.vector.tensor_copy(words[:], token_words[o][:].indirect(slot_offsets(first_expert, end_expert)))
+            for e in range(first_expert, end_expert):
+                slot_words[e, o] = words[:, (e - first_expert) * C : (e - first_expert + 1) * C]
 
         def gather_scales():
             for q in range(P // QUADRANT):
@@ -102,27 +98,31 @@ def tile_moe_shr_lin_bias_kernel(tc, x_words, x_scales, w, b, gate, offs, out):
                     nc.tensor.transpose(bank[:, r, :], gate_row[:, m0 + r : m0 + r + 1].to_broadcast([P, P]), identity[:])
                 nc.scalar.activation(by_run[:, :, m0 : m0 + per_bank], bank[:].rearrange("q r p -> q p r"), COPY)
 
-        def load_weights(first, count, group, group_count, cast, tag=None):
+        def load_and_round(first, cast, target):
+            count = target.shape[1]
             raw = keep.tile([P, count, PACK, N], F32, name="raw%d" % first, tag="raw%d" % first, align_bytes=64)
-            nc.sync.dma_start(
-                raw[:],
-                w_rows[first * K_PASS : (first + count) * K_PASS, :].rearrange("(u p j) n -> p u j n", p=P, j=PACK),
-            )
-            if first == group:
-                name = "interleaved%d" % group
-                interleaved[group] = keep.tile([P, group_count, N, PACK], BF16, name=name, tag=tag or name, align_bytes=64)
-            cast(
-                interleaved[group][:, first - group : first - group + count].rearrange("p u (c i) j -> p u c j i", i=4),
-                raw[:].rearrange("p u j (c i) -> p u c j i", i=4),
+            rows = w_rows[first * K_PASS : (first + count) * K_PASS, :]
+            nc.sync.dma_start(raw[:], rows.rearrange("(u p j) n -> p u j n", p=P, j=PACK))
+            cast(target, raw[:])
+
+        def rounded_tile(pieces, tag):
+            return keep.tile([P, len(pieces), N, PACK], BF16, name="rounded%d" % pieces[0], tag=tag, align_bytes=64)
+
+        def quantize(pieces, rounded, tag):
+            codes = keep.tile([P, len(pieces) * N], U32, name="codes%d" % pieces[0], tag=tag, align_bytes=64)
+            scales = keep.tile([P, len(pieces) * N], U8, name="scales%d" % pieces[0], align_bytes=64)
+            nc.vector.quantize_mx(codes[:].bitcast(FP8X4), scales[:], rounded[:].rearrange("p u n j -> p (u n j)"))
+            for u, piece in enumerate(pieces):
+                w_codes[piece] = codes[:, u * N : (u + 1) * N]
+                w_scales[piece] = scales[:, u * N : (u + 1) * N]
+
+        def by_runs(copy):
+            return lambda target, source: copy(
+                target.rearrange("p u (c i) j -> p c u j i", i=4), source.rearrange("p u j (c i) -> p c u j i", i=4)
             )
 
-        def quantize_weights(first, count, tag):
-            codes = keep.tile([P, count * N], U32, name="codes%d" % first, tag=tag, align_bytes=64)
-            scales = keep.tile([P, count * N], U8, name="scales%d" % first, align_bytes=64)
-            nc.vector.quantize_mx(codes[:].bitcast(FP8X4), scales[:], interleaved[first][:].rearrange("p u n j -> p (u n j)"))
-            for u in range(count):
-                w_codes[first + u] = codes[:, u * N : (u + 1) * N]
-                w_scales[first + u] = scales[:, u * N : (u + 1) * N]
+        def cast_on_gpsimd(target, source):
+            nc.gpsimd.tensor_scalar(target, source.rearrange("p u j n -> p u n j"), 1.0, 0.0, MULT, ADD)
 
         def multiply(sums, piece, words, plane):
             o = piece % PASSES
@@ -143,62 +143,106 @@ def tile_moe_shr_lin_bias_kernel(tc, x_words, x_scales, w, b, gate, offs, out):
                     plane = token_scales[PACK * o :, cols] if o < LAST else token_scales_last[:, cols]
                     multiply(shared_sums[i][:], SHARED + o, token_words[o][:, cols], plane)
 
-        def routed_expert(e, staging):
+        def routed_expert(e, tag):
             slots = slice(e * C, (e + 1) * C)
             bank = psum_ring.tile([P, BANK // P, P], F32, name="bank")
             sums = bank[:].rearrange("q r p -> q (r p)")[:, :C]
-            for o in range(LAST):
-                multiply(sums, e * PASSES + o, slot_words[o][:, slots], slot_scales[PACK * o :, slots])
-            if e < HEAD:
-                words = slot_words_head[:, slots]
-            else:
-                words = slot_words_tail[:, (e - HEAD) * C : (e - HEAD + 1) * C]
-            multiply(sums, e * PASSES + LAST, words, slot_scales_last[:, slots])
-            y = keep.tile([P, C], F32, name="y%d" % e, tag="raw%d" % staging, align_bytes=64)
+            for o in range(PASSES):
+                plane = slot_scales[PACK * o :, slots] if o < LAST else slot_scales_last[:, slots]
+                multiply(sums, e * PASSES + o, slot_words[e, o], plane)
+            y = keep.tile([P, C], F32, name="y%d" % e, tag=tag, align_bytes=64)
             nc.vector.scalar_tensor_tensor(y[:], sums, bias[:, e : e + 1], gate_all[:, slots], ADD, MULT)
-            nc.scalar.activation(routed[:].indirect(slot_offsets(e, e + 1)), y[:], COPY)
+            if e < E - 1:
+                nc.scalar.activation(routed[:].indirect(slot_offsets(e, e + 1)), y[:], COPY)
+            return y
 
-        def load_and_quantize(first, count, cast, leaving=None):
-            load_weights(first, count, first, count, cast)
-            if leaving is not None:
-                routed_expert(leaving, first)
-            quantize_weights(first, count, "codes%d" % first)
+        cast_on_scalar = by_runs(nc.scalar.copy)
+        cast_on_vector = by_runs(nc.vector.tensor_copy)
 
-        gather_token_pass(0)
+        def cast_on_scalar_and_gpsimd(target, source):
+            cast_on_gpsimd(target[:, :1], source[:, :1])
+            cast_on_scalar(target[:, 1:], source[:, 1:])
+
+        pieces = {}
+        rounded = {}
+        for e in range(E):
+            riding = [SHARED + HOSTS.index(e)] if e in HOSTS else []
+            pieces[e, 0] = list(range(e * PASSES, e * PASSES + FIRST_LOAD)) + riding
+            pieces[e, 1] = list(range(e * PASSES + FIRST_LOAD, (e + 1) * PASSES))
+            if e != EARLY_EXPERTS:
+                rounded[e, 0] = rounded_tile(pieces[e, 0], "first%d" % e)
+
+        def load_first(e, cast):
+            load_and_round(pieces[e, 0][0], cast, rounded[e, 0][:, :FIRST_LOAD])
+
+        def load_second(e, cast, tag):
+            rounded[e, 1] = rounded_tile(pieces[e, 1], tag)
+            load_and_round(pieces[e, 1][0], cast, rounded[e, 1][:])
+
+        def quantize_expert(e, together):
+            quantize(pieces[e, 0], rounded[e, 0], "raw%d" % pieces[e, 1][0] if together else "codes%d" % e)
+            quantize(pieces[e, 1], rounded[e, 1], "more_codes%d" % e)
+
+        load_tokens(0)
+        nc.sync.dma_start(offsets[:], offs)
+        gather_words(0, 0, E, "words0")
         spread_gate()
-        nc.sync.dma_start(bias[:], b)
         gather_scales()
-        load_and_quantize(SHARED, EARLY_SHARED, nc.scalar.copy)
+        for o in range(EARLY_SHARED):
+            load_and_round(SHARED + o, cast_on_scalar, rounded[HOSTS[o], 0][:, FIRST_LOAD:])
+        for o in range(1, PASSES):
+            e = (o - 1) // 2
+            if o % 2:
+                load_first(e, cast_on_scalar)
+            else:
+                load_second(e, cast_on_scalar, "second%d" % e)
+                quantize_expert(e, False)
+            if o == LAST:
+                shift_last_plane(slot_scales_last, slot_scales)
+            load_tokens(o)
+            if o < LAST:
+                gather_words(o, 0, E, "words%d" % o)
+        gather_words(LAST, 0, 1, "last_words0")
+        gather_words(LAST, 1, EARLY_EXPERTS, "last_words1")
+
+        e = EARLY_EXPERTS - 1
+        load_first(e, cast_on_scalar)
+        load_second(e, cast_on_scalar_and_gpsimd, "second%d" % e)
+        nc.sync.dma_start(bias[:], b)
+        for done in range(e):
+            routed_expert(done, "y%d" % done)
+        quantize_expert(e, True)
+        gather_words(LAST, EARLY_EXPERTS, E, "first%d" % e)
+        rounded[3, 0] = rounded_tile(pieces[3, 0], "second2")
+        load_first(3, cast_on_gpsimd)
+        load_first(4, cast_on_scalar)
+        routed_expert(2, "y2")
         shared_passes([0])
+        load_second(3, cast_on_vector, "second3")
+        load_first(5, cast_on_scalar)
+        quantize_expert(3, True)
+        quantize(pieces[4, 0], rounded[4, 0], "second3")
+        load_second(4, cast_on_vector, "second2")
+        routed_expert(3, "raw%d" % pieces[4, 1][0])
+        quantize(pieces[4, 1], rounded[4, 1], "more_codes4")
+        load_second(5, cast_on_vector, "second2")
+        routed_expert(4, "y4")
+        shared_passes([1])
+        quantize_expert(5, True)
 
-        early = []
-        for e in range(SCALAR_EXPERTS):
-            early = early + [(e * PASSES, FIRST_LOAD), (e * PASSES + FIRST_LOAD, PASSES - FIRST_LOAD)]
-        for j, (first, count) in enumerate(early):
-            if 0 < j <= LAST:
-                gather_token_pass(j)
-                if j < EARLY_SHARED:
-                    shared_passes([j])
-                if j == LAST - 1:
-                    shift_last_plane(slot_scales_last, slot_scales)
-            load_and_quantize(first, count, nc.scalar.copy, j - LAST if j >= LAST else None)
-
-        for e in range(SCALAR_EXPERTS, E):
-            first = e * PASSES
-            load_weights(first, 1, first, 1 + PAIR, nc.scalar.copy)
-            load_weights(first + 1, PAIR, first, 1 + PAIR, nc.vector.tensor_copy)
-            routed_expert(e - 1, first + 1)
-            load_weights(first + 1 + PAIR, PAIR, first + 1 + PAIR, PAIR, nc.vector.tensor_copy)
-            quantize_weights(first, 1 + PAIR, "raw%d" % (first + 1 + PAIR))
-            quantize_weights(first + 1 + PAIR, PAIR, "codes%d" % (first + 1 + PAIR))
-
-        late = SHARED + EARLY_SHARED
-        load_and_quantize(late, PASSES - EARLY_SHARED - PAIR, nc.vector.tensor_copy, E - 1)
-        last_pair = SHARED + PASSES - PAIR
-        load_weights(last_pair, PAIR, last_pair, PAIR, nc.vector.tensor_copy, "interleaved%d" % late)
-        quantize_weights(last_pair, PAIR, "codes%d" % last_pair)
+        late = [SHARED + EARLY_SHARED]
+        rounded_late = rounded_tile(late, "first%d" % (E - 1))
+        load_and_round(late[0], cast_on_vector, rounded_late[:])
+        y_last = routed_expert(E - 1, "raw%d" % late[0])
+        quantize(late, rounded_late, "codes_late")
+        shared_passes([EARLY_SHARED])
+        last = list(range(late[0] + 1, SHARED + PASSES))
+        rounded_last = rounded_tile(last, "second2")
+        load_and_round(last[0], cast_on_vector, rounded_last[:])
+        quantize(last, rounded_last, "codes_last")
+        nc.vector.tensor_copy(routed[:].indirect(slot_offsets(E - 1, E)), y_last[:])
         shift_last_plane(token_scales_last, token_scales)
-        shared_passes(range(EARLY_SHARED, PASSES))
+        shared_passes(range(EARLY_SHARED + 1, PASSES))
 
         starts = list(range(0, T, BANK)) + [T - BANK // 2, T]
         for start, end in zip(starts, starts[1:]):

@@ -98,12 +98,14 @@ def tile_moe_shr_lin_bias_kernel(tc, x_words, x_scales, w, b, gate, offs, out):
                     nc.tensor.transpose(bank[:, r, :], gate_row[:, m0 + r : m0 + r + 1].to_broadcast([P, P]), identity[:])
                 nc.scalar.activation(by_run[:, :, m0 : m0 + per_bank], bank[:].rearrange("q r p -> q p r"), COPY)
 
-        def load_and_round(first, cast, target):
-            count = target.shape[1]
+        def load_weights(first, count):
             raw = keep.tile([P, count, PACK, N], F32, name="raw%d" % first, tag="raw%d" % first, align_bytes=64)
             rows = w_rows[first * K_PASS : (first + count) * K_PASS, :]
             nc.sync.dma_start(raw[:], rows.rearrange("(u p j) n -> p u j n", p=P, j=PACK))
-            cast(target, raw[:])
+            return raw
+
+        def load_and_round(first, cast, target):
+            cast(target, load_weights(first, target.shape[1])[:])
 
         def rounded_tile(pieces, tag):
             return keep.tile([P, len(pieces), N, PACK], BF16, name="rounded%d" % pieces[0], tag=tag, align_bytes=64)
@@ -186,11 +188,15 @@ def tile_moe_shr_lin_bias_kernel(tc, x_words, x_scales, w, b, gate, offs, out):
         load_tokens(0)
         nc.sync.dma_start(offsets[:], offs)
         gather_words(0, 0, E, "words0")
-        spread_gate()
+        load_tokens(1)
+        gather_words(1, 0, E, "words1")
         gather_scales()
+        spread_gate()
+        raw = load_weights(SHARED, EARLY_SHARED)
         for o in range(EARLY_SHARED):
-            load_and_round(SHARED + o, cast_on_scalar, rounded[HOSTS[o], 0][:, FIRST_LOAD:])
-        for o in range(1, PASSES):
+            cast_on_scalar(rounded[HOSTS[o], 0][:, FIRST_LOAD:], raw[:, o : o + 1])
+        load_first(0, cast_on_scalar)
+        for o in range(2, PASSES):
             e = (o - 1) // 2
             if o % 2:
                 load_first(e, cast_on_scalar)

@@ -123,9 +123,6 @@ def tile_moe_shr_lin_bias_kernel(tc, x_words, x_scales, w, b, gate, offs, out):
                 target.rearrange("p u (c i) j -> p c u j i", i=4), source.rearrange("p u j (c i) -> p c u j i", i=4)
             )
 
-        def cast_on_gpsimd(target, source):
-            nc.gpsimd.tensor_scalar(target, source.rearrange("p u j n -> p u n j"), 1.0, 0.0, MULT, ADD)
-
         def multiply(sums, piece, words, plane):
             o = piece % PASSES
             nc.tensor.matmul_mx(
@@ -161,8 +158,8 @@ def tile_moe_shr_lin_bias_kernel(tc, x_words, x_scales, w, b, gate, offs, out):
         cast_on_scalar = by_runs(nc.scalar.copy)
         cast_on_vector = by_runs(nc.vector.tensor_copy)
 
-        def cast_on_scalar_and_gpsimd(target, source):
-            cast_on_gpsimd(target[:, :1], source[:, :1])
+        def cast_on_scalar_and_vector(target, source):
+            cast_on_vector(target[:, :1], source[:, :1])
             cast_on_scalar(target[:, 1:], source[:, 1:])
 
         pieces = {}
@@ -213,14 +210,14 @@ def tile_moe_shr_lin_bias_kernel(tc, x_words, x_scales, w, b, gate, offs, out):
 
         e = EARLY_EXPERTS - 1
         load_first(e, cast_on_scalar)
-        load_second(e, cast_on_scalar_and_gpsimd, "second%d" % e)
+        load_second(e, cast_on_scalar_and_vector, "second%d" % e)
         nc.sync.dma_start(bias[:], b)
         for done in range(e):
             routed_expert(done, "y%d" % done)
         quantize_expert(e, True)
         gather_words(LAST, EARLY_EXPERTS, E, "first%d" % e)
         rounded[3, 0] = rounded_tile(pieces[3, 0], "second2")
-        load_first(3, cast_on_gpsimd)
+        load_first(3, cast_on_vector)
         load_first(4, cast_on_scalar)
         routed_expert(2, "y2")
         shared_passes([0])

@@ -29,9 +29,9 @@ PER_COLUMN = 16
 SHARED = E * PASSES
 GATE_RUN = SLOTS // P
 FIRST_LOAD = 2
-EARLY_EXPERTS = E // 2
+SCALAR_EXPERTS = 3
 EARLY_SHARED = 2
-HOSTS = (2, 4)
+HOSTS = (3, 4)
 
 
 def tile_moe_shr_lin_bias_kernel(tc, x_words, x_scales, w, b, gate, offs, out):
@@ -50,7 +50,8 @@ def tile_moe_shr_lin_bias_kernel(tc, x_words, x_scales, w, b, gate, offs, out):
         slot_scales = keep.tile([P, SLOTS], U8, name="slot_scales", align_bytes=64)
         slot_scales_last = keep.tile([P, SLOTS], U8, name="slot_scales_last", align_bytes=64)
         routed = keep.tile([P, T], F32, name="routed")
-        nc.vector.memset(token_scales[:].bitcast(I32), 0)
+        nc.gpsimd.memset(token_scales[QUADRANT : 2 * QUADRANT, :].bitcast(I32), 0)
+        nc.vector.memset(token_scales[2 * QUADRANT :, :].bitcast(I32), 0)
         nc.vector.memset(routed[:], 0.0)
 
         token_words = [keep.tile([P, T], U32, name="token_words%d" % o, align_bytes=64) for o in range(PASSES)]
@@ -58,6 +59,7 @@ def tile_moe_shr_lin_bias_kernel(tc, x_words, x_scales, w, b, gate, offs, out):
         bias = keep.tile([P, E + 1], F32, name="bias")
         gate_all = keep.tile([P, SLOTS], F32, name="gate_all")
         shared_sums = [psum_shared.tile([P, BANK], F32, name="shared_sums%d" % i) for i in range(T // BANK)]
+        gate_row = keep.tile([P, GATE_RUN], F32, name="gate_row")
         w_codes = {}
         w_scales = {}
 
@@ -75,19 +77,25 @@ def tile_moe_shr_lin_bias_kernel(tc, x_words, x_scales, w, b, gate, offs, out):
                 slot_words[e, o] = words[:, (e - first_expert) * C : (e - first_expert + 1) * C]
 
         def gather_scales():
+            nc.sync.dma_start(token_scales[PACK * LAST : QUADRANT, :].bitcast(I32), x_scales[LAST].bitcast(I32))
             for q in range(P // QUADRANT):
                 nc.sync.dma_start(
-                    token_scales[QUADRANT * q : QUADRANT * q + PACK * PASSES, :].bitcast(I32),
-                    x_scales[:, PACK * q : PACK * (q + 1), :].bitcast(I32),
+                    token_scales[QUADRANT * q : QUADRANT * q + PACK * LAST, :].bitcast(I32),
+                    x_scales[:LAST, PACK * q : PACK * (q + 1), :].bitcast(I32),
                 )
+                if q == 0:
+                    load_gate()
             nc.vector.tensor_copy(slot_scales[:], token_scales[:].indirect(offsets[:]))
 
         def shift_last_plane(target, source):
-            nc.sync.dma_start(target[: P - PACK * LAST, :].bitcast(I32), source[PACK * LAST :, :].bitcast(I32))
+            for q in range(P // QUADRANT):
+                rows = slice(PACK * (LAST + q), PACK * (LAST + q + 1))
+                nc.sync.dma_start(target[QUADRANT * q : QUADRANT * q + PACK, :].bitcast(I32), source[rows, :].bitcast(I32))
+
+        def load_gate():
+            nc.sync.dma_start(gate_row[:], gate[0].rearrange("(p m) -> p m", m=GATE_RUN))
 
         def spread_gate():
-            gate_row = keep.tile([P, GATE_RUN], F32, name="gate_row")
-            nc.sync.dma_start(gate_row[:], gate[0].rearrange("(p m) -> p m", m=GATE_RUN))
             identity = keep.tile([P, P], F32, name="identity")
             make_identity(nc, identity[:])
             by_run = gate_all[:].rearrange("q (p m) -> q p m", m=GATE_RUN)
@@ -151,100 +159,100 @@ def tile_moe_shr_lin_bias_kernel(tc, x_words, x_scales, w, b, gate, offs, out):
                 multiply(sums, e * PASSES + o, slot_words[e, o], plane)
             y = keep.tile([P, C], F32, name="y%d" % e, tag=tag, align_bytes=64)
             nc.vector.scalar_tensor_tensor(y[:], sums, bias[:, e : e + 1], gate_all[:, slots], ADD, MULT)
-            if e < E - 1:
-                nc.scalar.activation(routed[:].indirect(slot_offsets(e, e + 1)), y[:], COPY)
-            return y
+            nc.scalar.activation(routed[:].indirect(slot_offsets(e, e + 1)), y[:], COPY)
 
         cast_on_scalar = by_runs(nc.scalar.copy)
         cast_on_vector = by_runs(nc.vector.tensor_copy)
+        places = {}
+        groups = {}
 
-        def cast_on_scalar_and_vector(target, source):
-            cast_on_vector(target[:, :1], source[:, :1])
-            cast_on_scalar(target[:, 1:], source[:, 1:])
+        def plan_group(name, pieces, tag=None):
+            tile = rounded_tile(pieces, tag or "rounded%d" % pieces[0])
+            groups[name] = (pieces, tile)
+            for u, piece in enumerate(pieces):
+                places[piece] = (tile, u)
 
-        pieces = {}
-        rounded = {}
-        for e in range(E):
-            riding = [SHARED + HOSTS.index(e)] if e in HOSTS else []
-            pieces[e, 0] = list(range(e * PASSES, e * PASSES + FIRST_LOAD)) + riding
-            pieces[e, 1] = list(range(e * PASSES + FIRST_LOAD, (e + 1) * PASSES))
-            if e != EARLY_EXPERTS:
-                rounded[e, 0] = rounded_tile(pieces[e, 0], "first%d" % e)
+        def round_pieces(cast, raw, first, lo, hi):
+            tile, u = places[first + lo]
+            cast(tile[:, u : u + hi - lo], raw[:, lo:hi])
 
-        def load_first(e, cast):
-            load_and_round(pieces[e, 0][0], cast, rounded[e, 0][:, :FIRST_LOAD])
+        def quantize_group(name):
+            pieces, tile = groups[name]
+            quantize(pieces, tile, "codes%d" % pieces[0])
 
-        def load_second(e, cast, tag):
-            rounded[e, 1] = rounded_tile(pieces[e, 1], tag)
-            load_and_round(pieces[e, 1][0], cast, rounded[e, 1][:])
+        def load_round(cast, first, count):
+            round_pieces(cast, load_weights(first, count), first, 0, count)
 
-        def quantize_expert(e, together):
-            quantize(pieces[e, 0], rounded[e, 0], "raw%d" % pieces[e, 1][0] if together else "codes%d" % e)
-            quantize(pieces[e, 1], rounded[e, 1], "more_codes%d" % e)
+        def scalar_load(e, second):
+            first = e * PASSES + (FIRST_LOAD if second else 0)
+            count = PASSES - FIRST_LOAD if second else FIRST_LOAD
+            plan_group(first, list(range(first, first + count)))
+            load_round(cast_on_scalar, first, count)
+            quantize_group(first)
 
-        load_tokens(0)
+        def vector_load(first, count):
+            raw = load_weights(first, count)
+            parts = [(0, count - 1), (count - 1, count)] if count > 1 else [(0, 1)]
+            for lo, hi in parts:
+                if first + lo not in groups:
+                    plan_group(first + lo, list(range(first + lo, first + hi)))
+                round_pieces(cast_on_vector, raw, first, lo, hi)
+            for lo, hi in parts:
+                quantize_group(first + lo)
+
+        for o, e in enumerate(HOSTS):
+            plan_group(e * PASSES + LAST, [e * PASSES + LAST, SHARED + o])
+
         nc.sync.dma_start(offsets[:], offs)
-        gather_words(0, 0, E, "words0")
-        load_tokens(1)
-        gather_words(1, 0, E, "words1")
         gather_scales()
-        spread_gate()
+        load_tokens(0)
+        gather_words(0, 0, E, "words0")
         raw = load_weights(SHARED, EARLY_SHARED)
         for o in range(EARLY_SHARED):
-            cast_on_scalar(rounded[HOSTS[o], 0][:, FIRST_LOAD:], raw[:, o : o + 1])
-        load_first(0, cast_on_scalar)
-        for o in range(2, PASSES):
-            e = (o - 1) // 2
-            if o % 2:
-                load_first(e, cast_on_scalar)
-            else:
-                load_second(e, cast_on_scalar, "second%d" % e)
-                quantize_expert(e, False)
-            if o == LAST:
-                shift_last_plane(slot_scales_last, slot_scales)
-            load_tokens(o)
-            if o < LAST:
-                gather_words(o, 0, E, "words%d" % o)
-        gather_words(LAST, 0, 1, "last_words0")
-        gather_words(LAST, 1, EARLY_EXPERTS, "last_words1")
-
-        e = EARLY_EXPERTS - 1
-        load_first(e, cast_on_scalar)
-        load_second(e, cast_on_scalar_and_vector, "second%d" % e)
+            round_pieces(cast_on_scalar, raw, SHARED, o, o + 1)
+        spread_gate()
+        load_tokens(1)
+        gather_words(1, 0, E, "words1")
+        scalar_load(0, False)
+        scalar_load(0, True)
+        load_tokens(2)
+        gather_words(2, 0, E, "words2")
+        shift_last_plane(token_scales_last, token_scales)
+        scalar_load(1, False)
+        load_tokens(3)
+        gather_words(3, 0, E, "words3")
+        scalar_load(1, True)
+        load_tokens(LAST)
+        shift_last_plane(slot_scales_last, slot_scales)
+        gather_words(LAST, 0, E // 2, "last_words0")
+        gather_words(LAST, E // 2, E, "last_words1")
+        first = (SCALAR_EXPERTS - 1) * PASSES
+        for pair in (first, first + 2):
+            plan_group(pair, [pair, pair + 1])
+            load_round(cast_on_scalar, pair, 2)
+            quantize_group(pair)
+        plan_group(first + 4, [first + 4, first + 5])
+        load_round(cast_on_scalar, first + 4, 2)
+        quantize_group(first + 4)
         nc.sync.dma_start(bias[:], b)
-        for done in range(e):
+        for done in range(SCALAR_EXPERTS - 1):
             routed_expert(done, "y%d" % done)
-        quantize_expert(e, True)
-        gather_words(LAST, EARLY_EXPERTS, E, "first%d" % e)
-        rounded[3, 0] = rounded_tile(pieces[3, 0], "second2")
-        load_first(3, cast_on_vector)
-        load_first(4, cast_on_scalar)
+        vector_load(16, 2)
         routed_expert(2, "y2")
+        vector_load(18, 2)
+        routed_expert(3, "y3")
         shared_passes([0])
-        load_second(3, cast_on_vector, "second3")
-        load_first(5, cast_on_scalar)
-        quantize_expert(3, True)
-        quantize(pieces[4, 0], rounded[4, 0], "second3")
-        load_second(4, cast_on_vector, "second2")
-        routed_expert(3, "raw%d" % pieces[4, 1][0])
-        quantize(pieces[4, 1], rounded[4, 1], "more_codes4")
-        load_second(5, cast_on_vector, "second2")
+        vector_load(20, 2)
+        vector_load(22, 3)
         routed_expert(4, "y4")
         shared_passes([1])
-        quantize_expert(5, True)
-
-        late = [SHARED + EARLY_SHARED]
-        rounded_late = rounded_tile(late, "first%d" % (E - 1))
-        load_and_round(late[0], cast_on_vector, rounded_late[:])
-        y_last = routed_expert(E - 1, "raw%d" % late[0])
-        quantize(late, rounded_late, "codes_late")
+        vector_load(25, 2)
+        vector_load(27, 2)
+        vector_load(29, 1)
+        routed_expert(5, "y5")
+        vector_load(32, 1)
         shared_passes([EARLY_SHARED])
-        last = list(range(late[0] + 1, SHARED + PASSES))
-        rounded_last = rounded_tile(last, "second2")
-        load_and_round(last[0], cast_on_vector, rounded_last[:])
-        quantize(last, rounded_last, "codes_last")
-        nc.vector.tensor_copy(routed[:].indirect(slot_offsets(E - 1, E)), y_last[:])
-        shift_last_plane(token_scales_last, token_scales)
+        vector_load(33, 2)
         shared_passes(range(EARLY_SHARED + 1, PASSES))
 
         starts = list(range(0, T, BANK)) + [T - BANK // 2, T]

@@ -140,7 +140,7 @@ def tile_moe_shr_lin_bias_kernel(tc, x_words, x_scales, w, b, gate, offs, out):
                 rhs=words.bitcast(FP8X4),
                 rhs_scale=plane,
                 start=(o == 0),
-                stop=(o == LAST),
+                stop=(o == (LAST - 1 if piece >= SHARED else LAST)),
             )
 
         def shared_passes(passes):
@@ -194,14 +194,15 @@ def tile_moe_shr_lin_bias_kernel(tc, x_words, x_scales, w, b, gate, offs, out):
             raw = load_weights(first, count)
             parts = [(0, count - 1), (count - 1, count)] if count > 1 else [(0, 1)]
             for lo, hi in parts:
-                if first + lo not in groups:
+                if first + lo not in places:
                     plan_group(first + lo, list(range(first + lo, first + hi)))
                 round_pieces(cast_on_vector, raw, first, lo, hi)
-            for lo, hi in parts:
-                quantize_group(first + lo)
+            names = [name for name in groups if set(groups[name][0]) & set(range(first, first + count))]
+            for name in sorted(names):
+                quantize_group(name)
 
-        for o, e in enumerate(HOSTS):
-            plan_group(e * PASSES + LAST, [e * PASSES + LAST, SHARED + o])
+        plan_group(0, [0, 1, SHARED])
+        plan_group(24, [24, SHARED + 1])
 
         nc.sync.dma_start(offsets[:], offs)
         gather_scales()
@@ -213,11 +214,15 @@ def tile_moe_shr_lin_bias_kernel(tc, x_words, x_scales, w, b, gate, offs, out):
         spread_gate()
         load_tokens(1)
         gather_words(1, 0, E, "words1")
-        scalar_load(0, False)
-        scalar_load(0, True)
+        plan_group(2, [2, 3, 4])
+        raw = load_weights(0, PASSES)
+        round_pieces(cast_on_scalar, raw, 0, 0, 2)
+        quantize_group(0)
+        shared_passes([0])
+        round_pieces(cast_on_scalar, raw, 0, 2, PASSES)
+        quantize_group(2)
         load_tokens(2)
         gather_words(2, 0, E, "words2")
-        shift_last_plane(token_scales_last, token_scales)
         scalar_load(1, False)
         load_tokens(3)
         gather_words(3, 0, E, "words3")
@@ -241,7 +246,6 @@ def tile_moe_shr_lin_bias_kernel(tc, x_words, x_scales, w, b, gate, offs, out):
         routed_expert(2, "y2")
         vector_load(18, 2)
         routed_expert(3, "y3")
-        shared_passes([0])
         vector_load(20, 2)
         vector_load(22, 3)
         routed_expert(4, "y4")
@@ -252,10 +256,16 @@ def tile_moe_shr_lin_bias_kernel(tc, x_words, x_scales, w, b, gate, offs, out):
         routed_expert(5, "y5")
         vector_load(32, 1)
         shared_passes([EARLY_SHARED])
-        vector_load(33, 2)
-        shared_passes(range(EARLY_SHARED + 1, PASSES))
+        raw = load_weights(33, 2)
+        for u in (1, 0):
+            plan_group(33 + u, [33 + u])
+            round_pieces(cast_on_vector, raw, 33, u, u + 1)
+        for u in (1, 0):
+            quantize_group(33 + u)
+        shift_last_plane(token_scales_last, token_scales)
+        shared_passes([LAST, LAST - 1])
 
-        starts = list(range(0, T, BANK)) + [T - BANK // 2, T]
+        starts = list(range(0, T + 1, BANK))
         for start, end in zip(starts, starts[1:]):
             sums = shared_sums[start // BANK][:, start % BANK : start % BANK + end - start]
             result = keep.tile([P, end - start], F32, name="result%d" % start)

@@ -194,15 +194,14 @@ def tile_moe_shr_lin_bias_kernel(tc, x_words, x_scales, w, b, gate, offs, out):
             raw = load_weights(first, count)
             parts = [(0, count - 1), (count - 1, count)] if count > 1 else [(0, 1)]
             for lo, hi in parts:
-                if first + lo not in places:
+                if first + lo not in groups:
                     plan_group(first + lo, list(range(first + lo, first + hi)))
                 round_pieces(cast_on_vector, raw, first, lo, hi)
-            names = [name for name in groups if set(groups[name][0]) & set(range(first, first + count))]
-            for name in sorted(names):
-                quantize_group(name)
+            for lo, hi in parts:
+                quantize_group(first + lo)
 
-        plan_group(0, [0, 1, SHARED])
-        plan_group(24, [24, SHARED + 1])
+        for o, e in enumerate(HOSTS):
+            plan_group(e * PASSES + LAST, [e * PASSES + LAST, SHARED + o])
 
         nc.sync.dma_start(offsets[:], offs)
         gather_scales()
@@ -214,11 +213,11 @@ def tile_moe_shr_lin_bias_kernel(tc, x_words, x_scales, w, b, gate, offs, out):
         spread_gate()
         load_tokens(1)
         gather_words(1, 0, E, "words1")
+        plan_group(0, [0, 1])
         plan_group(2, [2, 3, 4])
         raw = load_weights(0, PASSES)
         round_pieces(cast_on_scalar, raw, 0, 0, 2)
         quantize_group(0)
-        shared_passes([0])
         round_pieces(cast_on_scalar, raw, 0, 2, PASSES)
         quantize_group(2)
         load_tokens(2)
@@ -246,6 +245,7 @@ def tile_moe_shr_lin_bias_kernel(tc, x_words, x_scales, w, b, gate, offs, out):
         routed_expert(2, "y2")
         vector_load(18, 2)
         routed_expert(3, "y3")
+        shared_passes([0])
         vector_load(20, 2)
         vector_load(22, 3)
         routed_expert(4, "y4")
@@ -265,7 +265,7 @@ def tile_moe_shr_lin_bias_kernel(tc, x_words, x_scales, w, b, gate, offs, out):
         shift_last_plane(token_scales_last, token_scales)
         shared_passes([LAST, LAST - 1])
 
-        starts = list(range(0, T + 1, BANK))
+        starts = list(range(0, T, BANK)) + [T - BANK // 2, T]
         for start, end in zip(starts, starts[1:]):
             sums = shared_sums[start // BANK][:, start % BANK : start % BANK + end - start]
             result = keep.tile([P, end - start], F32, name="result%d" % start)

@@ -190,18 +190,22 @@ def tile_moe_shr_lin_bias_kernel(tc, x_words, x_scales, w, b, gate, offs, out):
             load_round(cast_on_scalar, first, count)
             quantize_group(first)
 
-        def vector_load(first, count):
+        def vector_load(first, count, finished=None):
             raw = load_weights(first, count)
             parts = [(0, count - 1), (count - 1, count)] if count > 1 else [(0, 1)]
             for lo, hi in parts:
-                if first + lo not in groups:
+                if first + lo not in places:
                     plan_group(first + lo, list(range(first + lo, first + hi)))
                 round_pieces(cast_on_vector, raw, first, lo, hi)
-            for lo, hi in parts:
-                quantize_group(first + lo)
+            names = [name for name in groups if set(groups[name][0]) & set(range(first, first + count))]
+            for name in sorted(names):
+                quantize_group(name)
+                if finished is not None and name == min(names):
+                    routed_expert(finished, "raw%d" % first)
 
-        for o, e in enumerate(HOSTS):
-            plan_group(e * PASSES + LAST, [e * PASSES + LAST, SHARED + o])
+        plan_group(0, [0, 1, 30])
+        plan_group(10, [10, 11, 14, 15])
+        plan_group(24, [24, 31])
 
         nc.sync.dma_start(offsets[:], offs)
         gather_scales()
@@ -213,11 +217,11 @@ def tile_moe_shr_lin_bias_kernel(tc, x_words, x_scales, w, b, gate, offs, out):
         spread_gate()
         load_tokens(1)
         gather_words(1, 0, E, "words1")
-        plan_group(0, [0, 1])
         plan_group(2, [2, 3, 4])
         raw = load_weights(0, PASSES)
         round_pieces(cast_on_scalar, raw, 0, 0, 2)
         quantize_group(0)
+        shared_passes([0])
         round_pieces(cast_on_scalar, raw, 0, 2, PASSES)
         quantize_group(2)
         load_tokens(2)
@@ -230,35 +234,27 @@ def tile_moe_shr_lin_bias_kernel(tc, x_words, x_scales, w, b, gate, offs, out):
         shift_last_plane(slot_scales_last, slot_scales)
         gather_words(LAST, 0, E // 2, "last_words0")
         gather_words(LAST, E // 2, E, "last_words1")
-        first = (SCALAR_EXPERTS - 1) * PASSES
-        for pair in (first, first + 2):
-            plan_group(pair, [pair, pair + 1])
-            load_round(cast_on_scalar, pair, 2)
-            quantize_group(pair)
-        plan_group(first + 4, [first + 4, first + 5])
-        load_round(cast_on_scalar, first + 4, 2)
-        quantize_group(first + 4)
+        load_round(cast_on_scalar, 10, 2)
+        plan_group(12, list(range(12, 14)))
+        load_round(cast_on_scalar, 12, 2)
+        quantize_group(12)
+        load_round(cast_on_scalar, 14, 2)
         nc.sync.dma_start(bias[:], b)
-        for done in range(SCALAR_EXPERTS - 1):
-            routed_expert(done, "y%d" % done)
-        vector_load(16, 2)
-        routed_expert(2, "y2")
-        vector_load(18, 2)
-        routed_expert(3, "y3")
-        shared_passes([0])
-        vector_load(20, 2)
-        vector_load(22, 3)
-        routed_expert(4, "y4")
+        routed_expert(0, "y0")
+        routed_expert(1, "y1")
+        quantize_group(10)
+        vector_load(16, 3)
+        vector_load(19, 3, 2)
+        vector_load(22, 3, 3)
+        vector_load(25, 3, 4)
         shared_passes([1])
-        vector_load(25, 2)
-        vector_load(27, 2)
-        vector_load(29, 1)
+        vector_load(28, 2)
         routed_expert(5, "y5")
         vector_load(32, 1)
         shared_passes([EARLY_SHARED])
         raw = load_weights(33, 2)
         for u in (1, 0):
-            plan_group(33 + u, [33 + u])
+            plan_group(33 + u, [33 + u], None if u else "codes29")
             round_pieces(cast_on_vector, raw, 33, u, u + 1)
         for u in (1, 0):
             quantize_group(33 + u)

@@ -131,7 +131,7 @@ def tile_moe_shr_lin_bias_kernel(tc, x_words, x_scales, w, b, gate, offs, out):
                 target.rearrange("p u (c i) j -> p c u j i", i=4), source.rearrange("p u j (c i) -> p c u j i", i=4)
             )
 
-        def multiply(sums, piece, words, plane):
+        def multiply(sums, piece, words, plane, start):
             o = piece % PASSES
             nc.tensor.matmul_mx(
                 sums,
@@ -139,7 +139,7 @@ def tile_moe_shr_lin_bias_kernel(tc, x_words, x_scales, w, b, gate, offs, out):
                 lhsT_scale=w_scales[piece],
                 rhs=words.bitcast(FP8X4),
                 rhs_scale=plane,
-                start=(o == 0),
+                start=start,
                 stop=(o == (LAST - 1 if piece >= SHARED else LAST)),
             )
 
@@ -148,15 +148,16 @@ def tile_moe_shr_lin_bias_kernel(tc, x_words, x_scales, w, b, gate, offs, out):
                 cols = slice(i * BANK, (i + 1) * BANK)
                 for o in passes:
                     plane = token_scales[PACK * o :, cols] if o < LAST else token_scales_last[:, cols]
-                    multiply(shared_sums[i][:], SHARED + o, token_words[o][:, cols], plane)
+                    multiply(shared_sums[i][:], SHARED + o, token_words[o][:, cols], plane, o == 0)
 
         def routed_expert(e, tag):
             slots = slice(e * C, (e + 1) * C)
             bank = psum_ring.tile([P, BANK // P, P], F32, name="bank")
             sums = bank[:].rearrange("q r p -> q (r p)")[:, :C]
-            for o in range(PASSES):
+            order = (2, 3, 0, 1, LAST) if e == 2 else range(PASSES)
+            for o in order:
                 plane = slot_scales[PACK * o :, slots] if o < LAST else slot_scales_last[:, slots]
-                multiply(sums, e * PASSES + o, slot_words[e, o], plane)
+                multiply(sums, e * PASSES + o, slot_words[e, o], plane, o == order[0])
             y = keep.tile([P, C], F32, name="y%d" % e, tag=tag, align_bytes=64)
             nc.vector.scalar_tensor_tensor(y[:], sums, bias[:, e : e + 1], gate_all[:, slots], ADD, MULT)
             nc.scalar.activation(routed[:].indirect(slot_offsets(e, e + 1)), y[:], COPY)
@@ -203,7 +204,8 @@ def tile_moe_shr_lin_bias_kernel(tc, x_words, x_scales, w, b, gate, offs, out):
                 if finished is not None and name == min(names):
                     routed_expert(finished, "raw%d" % first)
 
-        plan_group(0, [0, 1, 30])
+        plan_group(0, [0, 1])
+        plan_group(18, [18, 30])
         plan_group(10, [10, 11, 14, 15])
         plan_group(24, [24, 31])
 
@@ -221,7 +223,6 @@ def tile_moe_shr_lin_bias_kernel(tc, x_words, x_scales, w, b, gate, offs, out):
         raw = load_weights(0, PASSES)
         round_pieces(cast_on_scalar, raw, 0, 0, 2)
         quantize_group(0)
-        shared_passes([0])
         round_pieces(cast_on_scalar, raw, 0, 2, PASSES)
         quantize_group(2)
         load_tokens(2)
@@ -244,7 +245,9 @@ def tile_moe_shr_lin_bias_kernel(tc, x_words, x_scales, w, b, gate, offs, out):
         routed_expert(1, "y1")
         quantize_group(10)
         vector_load(16, 3)
-        vector_load(19, 3, 2)
+        routed_expert(2, "y2")
+        vector_load(19, 3)
+        shared_passes([0])
         vector_load(22, 3, 3)
         vector_load(25, 3, 4)
         shared_passes([1])

@@ -45,7 +45,7 @@ def tile_moe_shr_lin_bias_kernel(tc, x_words, x_scales, w, b, gate, offs, out):
 
         offsets = keep.tile([P, SLOTS // PER_COLUMN], U16, name="offsets")
 
-        token_scales = keep.tile([P, T], U8, name="token_scales", align_bytes=64)
+        token_scales = keep.tile([P, T], U8, name="token_scales", align_bytes=256)
         token_scales_last = keep.tile([P, T], U8, name="token_scales_last", align_bytes=64)
         slot_scales = keep.tile([P, SLOTS], U8, name="slot_scales", align_bytes=64)
         slot_scales_last = keep.tile([P, SLOTS], U8, name="slot_scales_last", align_bytes=64)
@@ -54,7 +54,7 @@ def tile_moe_shr_lin_bias_kernel(tc, x_words, x_scales, w, b, gate, offs, out):
         nc.vector.memset(token_scales[2 * QUADRANT :, :].bitcast(I32), 0)
         nc.vector.memset(routed[:], 0.0)
 
-        token_words = [keep.tile([P, T], U32, name="token_words%d" % o, align_bytes=64) for o in range(PASSES)]
+        token_words = [keep.tile([P, T], U32, name="token_words%d" % o, align_bytes=256) for o in range(PASSES)]
         slot_words = {}
         bias = keep.tile([P, E + 1], F32, name="bias")
         gate_all = keep.tile([P, SLOTS], F32, name="gate_all")
@@ -107,7 +107,7 @@ def tile_moe_shr_lin_bias_kernel(tc, x_words, x_scales, w, b, gate, offs, out):
                 nc.scalar.activation(by_run[:, :, m0 : m0 + per_bank], bank[:].rearrange("q r p -> q p r"), COPY)
 
         def load_weights(first, count):
-            raw = keep.tile([P, count, PACK, N], F32, name="raw%d" % first, tag="raw%d" % first, align_bytes=64)
+            raw = keep.tile([P, count, PACK, N], F32, name="raw%d" % first, tag="raw%d" % first, align_bytes=256)
             rows = w_rows[first * K_PASS : (first + count) * K_PASS, :]
             nc.sync.dma_start(raw[:], rows.rearrange("(u p j) n -> p u j n", p=P, j=PACK))
             return raw
@@ -158,7 +158,7 @@ def tile_moe_shr_lin_bias_kernel(tc, x_words, x_scales, w, b, gate, offs, out):
             for o in order:
                 plane = slot_scales[PACK * o :, slots] if o < LAST else slot_scales_last[:, slots]
                 multiply(sums, e * PASSES + o, slot_words[e, o], plane, o == order[0])
-            y = keep.tile([P, C], F32, name="y%d" % e, tag=tag, align_bytes=64)
+            y = keep.tile([P, C], F32, name="y%d" % e, tag=tag, align_bytes=256)
             nc.vector.scalar_tensor_tensor(y[:], sums, bias[:, e : e + 1], gate_all[:, slots], ADD, MULT)
             nc.scalar.activation(routed[:].indirect(slot_offsets(e, e + 1)), y[:], COPY)
 
@@ -267,6 +267,6 @@ def tile_moe_shr_lin_bias_kernel(tc, x_words, x_scales, w, b, gate, offs, out):
         starts = list(range(0, T, BANK)) + [T - BANK // 2, T]
         for start, end in zip(starts, starts[1:]):
             sums = shared_sums[start // BANK][:, start % BANK : start % BANK + end - start]
-            result = keep.tile([P, end - start], F32, name="result%d" % start)
+            result = keep.tile([P, end - start], F32, name="result%d" % start, align_bytes=256)
             nc.vector.scalar_tensor_tensor(result[:], sums, bias[:, E : E + 1], routed[:, start:end], ADD, ADD)
             nc.sync.dma_start(out[:, start:end], result[:])

@@ -28,10 +28,9 @@ BANK = 512
 PER_COLUMN = 16
 SHARED = E * PASSES
 GATE_RUN = SLOTS // P
-FIRST_LOAD = 2
-SCALAR_EXPERTS = 3
-EARLY_SHARED = 2
-HOSTS = (3, 4)
+ALIGN = 256
+PIECE_RAW = PACK * N * 4
+PIECE_ROUNDED = PACK * N * 2
 
 
 def tile_moe_shr_lin_bias_kernel(tc, x_words, x_scales, w, b, gate, offs, out):
@@ -40,12 +39,12 @@ def tile_moe_shr_lin_bias_kernel(tc, x_words, x_scales, w, b, gate, offs, out):
 
     with ExitStack() as ctx:
         keep = ctx.enter_context(tc.tile_pool(name="keep", bufs=1))
+        turns = ctx.enter_context(tc.tile_pool(name="turns", bufs=1))
         psum_shared = ctx.enter_context(tc.psum_pool(name="psum_shared", bufs=1))
         psum_ring = ctx.enter_context(tc.psum_pool(name="psum_ring", bufs=4))
 
         offsets = keep.tile([P, SLOTS // PER_COLUMN], U16, name="offsets")
-
-        token_scales = keep.tile([P, T], U8, name="token_scales", align_bytes=256)
+        token_scales = keep.tile([P, T], U8, name="token_scales", align_bytes=ALIGN)
         token_scales_last = keep.tile([P, T], U8, name="token_scales_last", align_bytes=64)
         slot_scales = keep.tile([P, SLOTS], U8, name="slot_scales", align_bytes=64)
         slot_scales_last = keep.tile([P, SLOTS], U8, name="slot_scales_last", align_bytes=64)
@@ -54,7 +53,7 @@ def tile_moe_shr_lin_bias_kernel(tc, x_words, x_scales, w, b, gate, offs, out):
         nc.vector.memset(token_scales[2 * QUADRANT :, :].bitcast(I32), 0)
         nc.vector.memset(routed[:], 0.0)
 
-        token_words = [keep.tile([P, T], U32, name="token_words%d" % o, align_bytes=256) for o in range(PASSES)]
+        token_words = [keep.tile([P, T], U32, name="token_words%d" % o, align_bytes=ALIGN) for o in range(PASSES)]
         slot_words = {}
         bias = keep.tile([P, E + 1], F32, name="bias")
         gate_all = keep.tile([P, SLOTS], F32, name="gate_all")
@@ -62,6 +61,14 @@ def tile_moe_shr_lin_bias_kernel(tc, x_words, x_scales, w, b, gate, offs, out):
         gate_row = keep.tile([P, GATE_RUN], F32, name="gate_row")
         w_codes = {}
         w_scales = {}
+        banks = {}
+
+        def place(shape, dtype, name, at, align=64):
+            if at is None:
+                return keep.tile(shape, dtype, name=name, align_bytes=align)
+            if isinstance(at, str):
+                return keep.tile(shape, dtype, name=name, tag=at, align_bytes=ALIGN)
+            return turns.tile(shape, dtype, name=name, offset=at, align_bytes=ALIGN)
 
         def slot_offsets(first_expert, end_expert):
             return offsets[:, first_expert * C // PER_COLUMN : end_expert * C // PER_COLUMN]
@@ -69,9 +76,8 @@ def tile_moe_shr_lin_bias_kernel(tc, x_words, x_scales, w, b, gate, offs, out):
         def load_tokens(o):
             nc.sync.dma_start(token_words[o][:].bitcast(I32), x_words[o].rearrange("p t r -> p (t r)").bitcast(I32))
 
-        def gather_words(o, first_expert, end_expert, tag):
-            shape = [P, (end_expert - first_expert) * C]
-            words = keep.tile(shape, U32, name="words%d_%d" % (o, first_expert), tag=tag, align_bytes=64)
+        def gather_words(o, first_expert, end_expert, at=None):
+            words = place([P, (end_expert - first_expert) * C], U32, "words%d_%d" % (o, first_expert), at)
             nc.vector.tensor_copy(words[:], token_words[o][:].indirect(slot_offsets(first_expert, end_expert)))
             for e in range(first_expert, end_expert):
                 slot_words[e, o] = words[:, (e - first_expert) * C : (e - first_expert + 1) * C]
@@ -84,16 +90,13 @@ def tile_moe_shr_lin_bias_kernel(tc, x_words, x_scales, w, b, gate, offs, out):
                     x_scales[:LAST, PACK * q : PACK * (q + 1), :].bitcast(I32),
                 )
                 if q == 0:
-                    load_gate()
+                    nc.sync.dma_start(gate_row[:], gate[0].rearrange("(p m) -> p m", m=GATE_RUN))
             nc.vector.tensor_copy(slot_scales[:], token_scales[:].indirect(offsets[:]))
 
         def shift_last_plane(target, source):
             for q in range(P // QUADRANT):
                 rows = slice(PACK * (LAST + q), PACK * (LAST + q + 1))
                 nc.sync.dma_start(target[QUADRANT * q : QUADRANT * q + PACK, :].bitcast(I32), source[rows, :].bitcast(I32))
-
-        def load_gate():
-            nc.sync.dma_start(gate_row[:], gate[0].rearrange("(p m) -> p m", m=GATE_RUN))
 
         def spread_gate():
             identity = keep.tile([P, P], F32, name="identity")
@@ -106,33 +109,38 @@ def tile_moe_shr_lin_bias_kernel(tc, x_words, x_scales, w, b, gate, offs, out):
                     nc.tensor.transpose(bank[:, r, :], gate_row[:, m0 + r : m0 + r + 1].to_broadcast([P, P]), identity[:])
                 nc.scalar.activation(by_run[:, :, m0 : m0 + per_bank], bank[:].rearrange("q r p -> q p r"), COPY)
 
-        def load_weights(first, count):
-            raw = keep.tile([P, count, PACK, N], F32, name="raw%d" % first, tag="raw%d" % first, align_bytes=256)
+        def load_weights(first, count, at=None):
+            raw = place([P, count, PACK, N], F32, "raw%d" % first, at, ALIGN)
             rows = w_rows[first * K_PASS : (first + count) * K_PASS, :]
             nc.sync.dma_start(raw[:], rows.rearrange("(u p j) n -> p u j n", p=P, j=PACK))
             return raw
-
-        def load_and_round(first, cast, target):
-            cast(target, load_weights(first, target.shape[1])[:])
-
-        def rounded_tile(pieces, tag):
-            return keep.tile([P, len(pieces), N, PACK], BF16, name="rounded%d" % pieces[0], tag=tag, align_bytes=64)
-
-        def quantize(pieces, rounded, tag):
-            codes = keep.tile([P, len(pieces) * N], U32, name="codes%d" % pieces[0], tag=tag, align_bytes=64)
-            scales = keep.tile([P, len(pieces) * N], U8, name="scales%d" % pieces[0], align_bytes=64)
-            nc.vector.quantize_mx(codes[:].bitcast(FP8X4), scales[:], rounded[:].rearrange("p u n j -> p (u n j)"))
-            for u, piece in enumerate(pieces):
-                w_codes[piece] = codes[:, u * N : (u + 1) * N]
-                w_scales[piece] = scales[:, u * N : (u + 1) * N]
 
         def by_runs(copy):
             return lambda target, source: copy(
                 target.rearrange("p u (c i) j -> p c u j i", i=4), source.rearrange("p u j (c i) -> p c u j i", i=4)
             )
 
-        def multiply(sums, piece, words, plane, start):
-            o = piece % PASSES
+        on_scalar = by_runs(nc.scalar.copy)
+        on_vector = by_runs(nc.vector.tensor_copy)
+
+        def on_gpsimd(target, source):
+            nc.gpsimd.tensor_scalar(target, source.rearrange("p u j n -> p u n j"), 1.0, 0.0, MULT, ADD)
+
+        def round_pieces(cast, first, raw, at=None):
+            rounded = place([P, raw.shape[1], N, PACK], BF16, "rounded%d" % first, at)
+            cast(rounded[:], raw)
+            return rounded
+
+        def quantize(pieces, rounded, at=None, scales_at=None):
+            first, count = pieces[0], len(pieces)
+            codes = place([P, count * N], U32, "codes%d" % first, at)
+            scales = place([P, count * N], U8, "scales%d" % first, scales_at)
+            nc.vector.quantize_mx(codes[:].bitcast(FP8X4), scales[:], rounded[:].rearrange("p u n j -> p (u n j)"))
+            for u, piece in enumerate(pieces):
+                w_codes[piece] = codes[:, u * N : (u + 1) * N]
+                w_scales[piece] = scales[:, u * N : (u + 1) * N]
+
+        def multiply(sums, piece, words, plane, start, stop):
             nc.tensor.matmul_mx(
                 sums,
                 lhsT=w_codes[piece].bitcast(FP8X4),
@@ -140,133 +148,129 @@ def tile_moe_shr_lin_bias_kernel(tc, x_words, x_scales, w, b, gate, offs, out):
                 rhs=words.bitcast(FP8X4),
                 rhs_scale=plane,
                 start=start,
-                stop=(o == (LAST - 1 if piece >= SHARED else LAST)),
+                stop=stop,
             )
 
-        def shared_passes(passes):
+        def shared_passes(passes, first, last):
             for i in range(T // BANK):
                 cols = slice(i * BANK, (i + 1) * BANK)
                 for o in passes:
                     plane = token_scales[PACK * o :, cols] if o < LAST else token_scales_last[:, cols]
-                    multiply(shared_sums[i][:], SHARED + o, token_words[o][:, cols], plane, o == 0)
+                    multiply(shared_sums[i][:], SHARED + o, token_words[o][:, cols], plane, o == first, o == last)
 
-        def routed_expert(e, tag):
+        def expert_product(e, order, part=slice(None)):
             slots = slice(e * C, (e + 1) * C)
-            bank = psum_ring.tile([P, BANK // P, P], F32, name="bank")
-            sums = bank[:].rearrange("q r p -> q (r p)")[:, :C]
-            order = (2, 3, 0, 1, LAST) if e == 2 else range(PASSES)
-            for o in order:
+            if e not in banks:
+                bank = psum_ring.tile([P, BANK // P, P], F32, name="bank")
+                banks[e] = bank[:].rearrange("q r p -> q (r p)")[:, :C]
+            for o in order[part]:
                 plane = slot_scales[PACK * o :, slots] if o < LAST else slot_scales_last[:, slots]
-                multiply(sums, e * PASSES + o, slot_words[e, o], plane, o == order[0])
-            y = keep.tile([P, C], F32, name="y%d" % e, tag=tag, align_bytes=256)
-            nc.vector.scalar_tensor_tensor(y[:], sums, bias[:, e : e + 1], gate_all[:, slots], ADD, MULT)
+                multiply(banks[e], e * PASSES + o, slot_words[e, o], plane, o == order[0], o == order[-1])
+
+        def expert_result(e, at=None, column=None):
+            slots = slice(e * C, (e + 1) * C)
+            y = place([P, C], F32, "y%d" % e, at)
+            nc.vector.scalar_tensor_tensor(y[:], banks[e], bias[:, e : e + 1] if column is None else column, gate_all[:, slots], ADD, MULT)
             nc.scalar.activation(routed[:].indirect(slot_offsets(e, e + 1)), y[:], COPY)
-
-        cast_on_scalar = by_runs(nc.scalar.copy)
-        cast_on_vector = by_runs(nc.vector.tensor_copy)
-        places = {}
-        groups = {}
-
-        def plan_group(name, pieces, tag=None):
-            tile = rounded_tile(pieces, tag or "rounded%d" % pieces[0])
-            groups[name] = (pieces, tile)
-            for u, piece in enumerate(pieces):
-                places[piece] = (tile, u)
-
-        def round_pieces(cast, raw, first, lo, hi):
-            tile, u = places[first + lo]
-            cast(tile[:, u : u + hi - lo], raw[:, lo:hi])
-
-        def quantize_group(name):
-            pieces, tile = groups[name]
-            quantize(pieces, tile, "codes%d" % pieces[0])
-
-        def load_round(cast, first, count):
-            round_pieces(cast, load_weights(first, count), first, 0, count)
-
-        def scalar_load(e, second):
-            first = e * PASSES + (FIRST_LOAD if second else 0)
-            count = PASSES - FIRST_LOAD if second else FIRST_LOAD
-            plan_group(first, list(range(first, first + count)))
-            load_round(cast_on_scalar, first, count)
-            quantize_group(first)
-
-        def vector_load(first, count, finished=None):
-            raw = load_weights(first, count)
-            parts = [(0, count - 1), (count - 1, count)] if count > 1 else [(0, 1)]
-            for lo, hi in parts:
-                if first + lo not in places:
-                    plan_group(first + lo, list(range(first + lo, first + hi)))
-                round_pieces(cast_on_vector, raw, first, lo, hi)
-            names = [name for name in groups if set(groups[name][0]) & set(range(first, first + count))]
-            for name in sorted(names):
-                quantize_group(name)
-                if finished is not None and name == min(names):
-                    routed_expert(finished, "raw%d" % first)
-
-        plan_group(0, [0, 1])
-        plan_group(18, [18, 30])
-        plan_group(10, [10, 11, 14, 15])
-        plan_group(24, [24, 31])
 
         nc.sync.dma_start(offsets[:], offs)
         gather_scales()
         load_tokens(0)
-        gather_words(0, 0, E, "words0")
-        raw = load_weights(SHARED, EARLY_SHARED)
-        for o in range(EARLY_SHARED):
-            round_pieces(cast_on_scalar, raw, SHARED, o, o + 1)
+        gather_words(0, 0, E)
+        raw = load_weights(SHARED, 2, "early0")
         spread_gate()
+        hosts = [place([P, 2, N, PACK], BF16, "host%d" % o, None) for o in range(2)]
+        for o in range(2):
+            on_scalar(hosts[o][:, 1:], raw[:, o : o + 1])
         load_tokens(1)
-        gather_words(1, 0, E, "words1")
-        plan_group(2, [2, 3, 4])
+        gather_words(1, 0, E)
         raw = load_weights(0, PASSES)
-        round_pieces(cast_on_scalar, raw, 0, 0, 2)
-        quantize_group(0)
-        round_pieces(cast_on_scalar, raw, 0, 2, PASSES)
-        quantize_group(2)
+        quantize([0, 1], round_pieces(on_scalar, 0, raw[:, :2]))
+        triple = round_pieces(on_scalar, 2, raw[:, 2:])
         load_tokens(2)
-        gather_words(2, 0, E, "words2")
-        scalar_load(1, False)
+        nc.sync.dma_start(bias[:], b)
+        KIB = 1024
+        own_bias = []
+        for e, (at, size) in enumerate(((2 * KIB, 768), (8 * KIB, 64), (10 * KIB, 64), (12 * KIB, 64))):
+            own_bias.append(place([P, size], F32, "own_bias%d" % e, at))
+            nc.scalar.copy(own_bias[e][:, :1], bias[:, e : e + 1])
+        gather_words(2, 0, E)
+        quantize([2, 3, 4], triple)
+        quantize([5, 6], round_pieces(on_scalar, 5, load_weights(5, 2, "early1")[:]))
         load_tokens(3)
-        gather_words(3, 0, E, "words3")
-        scalar_load(1, True)
+        gather_words(3, 0, E)
+        quantize([7, 8, 9], round_pieces(on_scalar, 7, load_weights(7, 3)[:]))
+        four = place([P, 4, N, PACK], BF16, "rounded10", None)
+        on_scalar(four[:, :2], load_weights(10, 2)[:])
+        for e in (0, 1):
+            expert_product(e, range(PASSES), slice(LAST))
         load_tokens(LAST)
         shift_last_plane(slot_scales_last, slot_scales)
-        gather_words(LAST, 0, E // 2, "last_words0")
-        gather_words(LAST, E // 2, E, "last_words1")
-        load_round(cast_on_scalar, 10, 2)
-        plan_group(12, list(range(12, 14)))
-        load_round(cast_on_scalar, 12, 2)
-        quantize_group(12)
-        load_round(cast_on_scalar, 14, 2)
-        nc.sync.dma_start(bias[:], b)
-        routed_expert(0, "y0")
-        routed_expert(1, "y1")
-        quantize_group(10)
-        vector_load(16, 3)
-        routed_expert(2, "y2")
-        vector_load(19, 3)
-        shared_passes([0])
-        vector_load(22, 3, 3)
-        vector_load(25, 3, 4)
-        shared_passes([1])
-        vector_load(28, 2)
-        routed_expert(5, "y5")
-        vector_load(32, 1)
-        shared_passes([EARLY_SHARED])
-        raw = load_weights(33, 2)
-        for u in (1, 0):
-            plan_group(33 + u, [33 + u], None if u else "codes29")
-            round_pieces(cast_on_vector, raw, 33, u, u + 1)
-        for u in (1, 0):
-            quantize_group(33 + u)
+        gather_words(LAST, 0, 2)
+        gather_words(LAST, 2, 4)
+        for e in (0, 1):
+            expert_product(e, range(PASSES), slice(LAST, None))
+        on_scalar(four[:, 2:3], load_weights(12, 1)[:])
+        on_scalar(four[:, 3:], load_weights(13, 1, 14 * KIB)[:])
+        on_scalar(hosts[0][:, :1], load_weights(14, 1)[:])
+        expert_result(0, 14 * KIB, own_bias[0][:, :1])
+        between = [place([P, 2, N, PACK], BF16, "rounded15", 2816)]
+        on_scalar(between[0][:, :1], load_weights(15, 1)[:])
+        expert_result(1, 15 * KIB, own_bias[1][:, :1])
+        between.append(round_pieces(on_scalar, 16, load_weights(16, 1)[:], 8 * KIB))
+        raw20 = load_weights(20, 1)
+        gather_words(LAST, 4, E, 256)
+        quantize([10, 11, 12, 13], four, 4864)
+        quantize([14, SHARED], hosts[0], None, 2304)
+        expert_product(2, range(PASSES))
+        shared_passes([0], 0, None)
+        raw = load_weights(17, 3, 16 * KIB)
+        pair = round_pieces(on_vector, 17, raw[:, :2])
+        on_vector(between[0][:, 1:], raw[:, 2:])
+        quantize([17, 18], pair)
+        expert_result(2, 16 * KIB, own_bias[2][:, :1])
+        between.append(round_pieces(on_scalar, 20, raw20[:], 10 * KIB))
+        quantize([15, 19], between[0])
+        pair = round_pieces(on_vector, 21, load_weights(21, 2, 22 * KIB)[:])
+        quantize([16], between[1], 17 * KIB)
+        expert_product(3, (2, 3, 0, 4, 1))
+        raw25 = load_weights(25, 1)
+        raw = load_weights(23, 2, 26 * KIB)
+        single = round_pieces(on_vector, 23, raw[:, :1])
+        on_vector(hosts[1][:, :1], raw[:, 1:])
+        quantize([21, 22], pair)
+        expert_result(3, 26 * KIB, own_bias[3][:, :1])
+        between.append(round_pieces(on_scalar, 25, raw25[:], 12 * KIB))
+        quantize([23], single)
+        quantize([24, SHARED + 1], hosts[1])
+        quantize([20], between[2], 27 * KIB)
+        expert_product(4, (1, 2, 3, 4, 0))
+        shared_passes([1], 0, None)
+        raw = load_weights(26, 3, 30 * KIB)
+        pair = round_pieces(on_vector, 26, raw[:, :2])
+        last = [round_pieces(on_vector, 28, raw[:, 2:])]
+        quantize([26, 27], pair)
+        expert_result(4, 30 * KIB)
+        last.append(round_pieces(on_vector, 29, load_weights(29, 1, "early0")[:]))
+        quantize([28], last[0])
+        quantize([25], between[3], "early0")
+        quantize([29], last[1], "codes29")
+        expert_product(5, (1, 2, 3, 0, 4))
+        single = round_pieces(on_vector, 32, load_weights(32, 1)[:])
+        raw = load_weights(33, 2, "early1")
+        last = [round_pieces(on_vector, 34, raw[:, 1:])]
+        expert_result(E - 1)
+        quantize([32], single)
+        shared_passes([2], 0, None)
+        last.append(round_pieces(on_vector, 33, raw[:, :1], "codes29"))
+        quantize([34], last[0])
+        quantize([33], last[1])
         shift_last_plane(token_scales_last, token_scales)
-        shared_passes([LAST, LAST - 1])
+        shared_passes([LAST, 3], 0, 3)
 
         starts = list(range(0, T, BANK)) + [T - BANK // 2, T]
         for start, end in zip(starts, starts[1:]):
             sums = shared_sums[start // BANK][:, start % BANK : start % BANK + end - start]
-            result = keep.tile([P, end - start], F32, name="result%d" % start, align_bytes=256)
+            result = keep.tile([P, end - start], F32, name="result%d" % start, align_bytes=ALIGN)
             nc.vector.scalar_tensor_tensor(result[:], sums, bias[:, E : E + 1], routed[:, start:end], ADD, ADD)
             nc.sync.dma_start(out[:, start:end], result[:])

@@ -173,35 +173,35 @@ def tile_moe_shr_lin_bias_kernel(tc, x_words, x_scales, w, b, gate, offs, out):
             nc.vector.scalar_tensor_tensor(y[:], banks[e], bias[:, e : e + 1] if column is None else column, gate_all[:, slots], ADD, MULT)
             nc.scalar.activation(routed[:].indirect(slot_offsets(e, e + 1)), y[:], COPY)
 
+        KIB = 1024
         nc.sync.dma_start(offsets[:], offs)
         gather_scales()
         load_tokens(0)
         gather_words(0, 0, E)
+        load_tokens(1)
+        gather_words(1, 0, E)
         raw = load_weights(SHARED, 2, "early0")
         spread_gate()
         hosts = [place([P, 2, N, PACK], BF16, "host%d" % o, None) for o in range(2)]
         for o in range(2):
             on_scalar(hosts[o][:, 1:], raw[:, o : o + 1])
-        load_tokens(1)
-        gather_words(1, 0, E)
+        load_tokens(2)
+        gather_words(2, 0, E)
         raw = load_weights(0, PASSES)
         quantize([0, 1], round_pieces(on_scalar, 0, raw[:, :2]))
         triple = round_pieces(on_scalar, 2, raw[:, 2:])
-        load_tokens(2)
         nc.sync.dma_start(bias[:], b)
-        KIB = 1024
         own_bias = []
-        for e, (at, size) in enumerate(((2 * KIB, 768), (8 * KIB, 64), (10 * KIB, 64), (12 * KIB, 64))):
-            own_bias.append(place([P, size], F32, "own_bias%d" % e, at))
-            nc.scalar.copy(own_bias[e][:, :1], bias[:, e : e + 1])
-        gather_words(2, 0, E)
-        quantize([2, 3, 4], triple)
-        quantize([5, 6], round_pieces(on_scalar, 5, load_weights(5, 2, "early1")[:]))
+        for e, at in ((0, 0), (3, 15 * KIB)):
+            own_bias.append(place([P, 8], F32, "own_bias%d" % e, at))
+            nc.scalar.copy(own_bias[-1][:, :1], bias[:, e : e + 1])
         load_tokens(3)
         gather_words(3, 0, E)
+        quantize([2, 3, 4], triple)
+        quantize([5, 6], round_pieces(on_scalar, 5, load_weights(5, 2, "early1")[:]))
         quantize([7, 8, 9], round_pieces(on_scalar, 7, load_weights(7, 3)[:]))
-        four = place([P, 4, N, PACK], BF16, "rounded10", None)
-        on_scalar(four[:, :2], load_weights(10, 2)[:])
+        four = place([P, 4, N, PACK], BF16, "rounded10", "rounded10")
+        on_scalar(four[:, :1], load_weights(10, 1)[:])
         for e in (0, 1):
             expert_product(e, range(PASSES), slice(LAST))
         load_tokens(LAST)
@@ -210,59 +210,64 @@ def tile_moe_shr_lin_bias_kernel(tc, x_words, x_scales, w, b, gate, offs, out):
         gather_words(LAST, 2, 4)
         for e in (0, 1):
             expert_product(e, range(PASSES), slice(LAST, None))
-        on_scalar(four[:, 2:3], load_weights(12, 1)[:])
-        on_scalar(four[:, 3:], load_weights(13, 1, 14 * KIB)[:])
-        on_scalar(hosts[0][:, :1], load_weights(14, 1)[:])
-        expert_result(0, 14 * KIB, own_bias[0][:, :1])
-        between = [place([P, 2, N, PACK], BF16, "rounded15", 2816)]
+        on_scalar(four[:, 1:2], load_weights(11, 1)[:])
+        on_scalar(four[:, 2:3], load_weights(12, 1, 2 * KIB)[:])
+        on_scalar(four[:, 3:], load_weights(13, 1)[:])
+        fifth = round_pieces(on_scalar, 14, load_weights(14, 1)[:])
+        expert_result(0, 2 * KIB, own_bias[0][:, :1])
+        between = [place([P, 2, N, PACK], BF16, "rounded15", 0)]
         on_scalar(between[0][:, :1], load_weights(15, 1)[:])
-        expert_result(1, 15 * KIB, own_bias[1][:, :1])
-        between.append(round_pieces(on_scalar, 16, load_weights(16, 1)[:], 8 * KIB))
-        raw20 = load_weights(20, 1)
-        gather_words(LAST, 4, E, 256)
-        quantize([10, 11, 12, 13], four, 4864)
-        quantize([14, SHARED], hosts[0], None, 2304)
+        gather_words(LAST, 4, E, 3 * KIB)
+        quantize([10, 11, 12, 13], four)
+        quantize([14], fifth)
         expert_product(2, range(PASSES))
-        shared_passes([0], 0, None)
-        raw = load_weights(17, 3, 16 * KIB)
-        pair = round_pieces(on_vector, 17, raw[:, :2])
-        on_vector(between[0][:, 1:], raw[:, 2:])
-        quantize([17, 18], pair)
-        expert_result(2, 16 * KIB, own_bias[2][:, :1])
-        between.append(round_pieces(on_scalar, 20, raw20[:], 10 * KIB))
+        expert_result(1, "rounded10")
+        raw = load_weights(16, 3, 5 * KIB)
+        pair = round_pieces(on_vector, 16, raw[:, :2])
+        on_vector(hosts[0][:, :1], raw[:, 2:])
+        on_vector(between[0][:, 1:], load_weights(19, 1)[:])
+        quantize([16, 17], pair)
+        expert_result(2, 5 * KIB)
         quantize([15, 19], between[0])
-        pair = round_pieces(on_vector, 21, load_weights(21, 2, 22 * KIB)[:])
-        quantize([16], between[1], 17 * KIB)
-        expert_product(3, (2, 3, 0, 4, 1))
-        raw25 = load_weights(25, 1)
-        raw = load_weights(23, 2, 26 * KIB)
-        single = round_pieces(on_vector, 23, raw[:, :1])
+        quantize([18, SHARED], hosts[0])
+        expert_product(3, (1, 2, 0, 4, 3))
+        shared_passes([0], 0, None)
+        raw = load_weights(20, 3, "raw20")
+        pair = round_pieces(on_vector, 20, raw[:, :2])
+        pair2 = place([P, 2, N, PACK], BF16, "rounded22", None)
+        on_vector(pair2[:, :1], raw[:, 2:])
+        between.append(round_pieces(on_scalar, 25, load_weights(25, 1)[:]))
+        raw = load_weights(23, 2)
+        quantize([20, 21], pair)
+        expert_result(3, "raw20", own_bias[1][:, :1])
+        on_vector(pair2[:, 1:], raw[:, :1])
         on_vector(hosts[1][:, :1], raw[:, 1:])
-        quantize([21, 22], pair)
-        expert_result(3, 26 * KIB, own_bias[3][:, :1])
-        between.append(round_pieces(on_scalar, 25, raw25[:], 12 * KIB))
-        quantize([23], single)
+        quantize([22, 23], pair2)
         quantize([24, SHARED + 1], hosts[1])
-        quantize([20], between[2], 27 * KIB)
-        expert_product(4, (1, 2, 3, 4, 0))
+        expert_product(4, range(PASSES))
         shared_passes([1], 0, None)
-        raw = load_weights(26, 3, 30 * KIB)
-        pair = round_pieces(on_vector, 26, raw[:, :2])
-        last = [round_pieces(on_vector, 28, raw[:, 2:])]
-        quantize([26, 27], pair)
-        expert_result(4, 30 * KIB)
-        last.append(round_pieces(on_vector, 29, load_weights(29, 1, "early0")[:]))
-        quantize([28], last[0])
-        quantize([25], between[3], "early0")
-        quantize([29], last[1], "codes29")
-        expert_product(5, (1, 2, 3, 0, 4))
-        single = round_pieces(on_vector, 32, load_weights(32, 1)[:])
+        raw = load_weights(26, 2, 11 * KIB)
+        single = round_pieces(on_vector, 26, raw[:, :1])
+        pair = place([P, 2, N, PACK], BF16, "rounded27", None)
+        on_vector(pair[:, :1], raw[:, 1:])
+        late = place([P, 1, N, PACK], BF16, "rounded29", 15 * KIB)
+        on_scalar(late[:], load_weights(29, 1)[:])
+        raw28 = load_weights(28, 1, "early0")
+        between.append(late)
+        quantize([26], single)
+        expert_result(4, 11 * KIB)
+        on_vector(pair[:, 1:], raw28[:])
+        quantize([25], between[1], 12 * KIB)
+        quantize([27, 28], pair)
+        quantize([29], between[2], "early0")
+        expert_product(5, (1, 0, 2, 3, 4))
+        third = round_pieces(on_vector, 32, load_weights(32, 1)[:])
         raw = load_weights(33, 2, "early1")
         last = [round_pieces(on_vector, 34, raw[:, 1:])]
         expert_result(E - 1)
-        quantize([32], single)
+        quantize([32], third)
         shared_passes([2], 0, None)
-        last.append(round_pieces(on_vector, 33, raw[:, :1], "codes29"))
+        last.append(round_pieces(on_vector, 33, raw[:, :1], "early0"))
         quantize([34], last[0])
         quantize([33], last[1])
         shift_last_plane(token_scales_last, token_scales)

from contextlib import ExitStack

import concourse.mybir as mybir
from concourse.masks import make_identity

K, T, E, C, N = 2560, 2048, 6, 256, 128
SLOTS = E * C
FLOPS = 2 * K * N * (T + SLOTS)

F32 = mybir.dt.float32
BF16 = mybir.dt.bfloat16
I32 = mybir.dt.int32
U32 = mybir.dt.uint32
U16 = mybir.dt.uint16
U8 = mybir.dt.uint8
FP8X4 = mybir.dt.float8_e4m3fn_x4
ADD = mybir.AluOpType.add
MULT = mybir.AluOpType.mult
COPY = mybir.ActivationFunctionType.Copy

P = 128
QUADRANT = 32
PACK = 4
K_PASS = P * PACK
PASSES = K // K_PASS
LAST = PASSES - 1
BANK = 512
PER_COLUMN = 16
SHARED = E * PASSES
GATE_RUN = SLOTS // P
ALIGN = 256
PIECE_RAW = PACK * N * 4
PIECE_ROUNDED = PACK * N * 2


def tile_moe_shr_lin_bias_kernel(tc, x_words, x_scales, w, b, gate, offs, out):
    nc = tc.nc
    w_rows = w.rearrange("e k n -> (e k) n")

    with ExitStack() as ctx:
        keep = ctx.enter_context(tc.tile_pool(name="keep", bufs=1))
        turns = ctx.enter_context(tc.tile_pool(name="turns", bufs=1))
        psum_shared = ctx.enter_context(tc.psum_pool(name="psum_shared", bufs=1))
        psum_ring = ctx.enter_context(tc.psum_pool(name="psum_ring", bufs=4))

        offsets = keep.tile([P, SLOTS // PER_COLUMN], U16, name="offsets")
        token_scales = keep.tile([P, T], U8, name="token_scales", align_bytes=ALIGN)
        token_scales_last = keep.tile([P, T], U8, name="token_scales_last", align_bytes=64)
        slot_scales = keep.tile([P, SLOTS], U8, name="slot_scales", align_bytes=64)
        slot_scales_last = keep.tile([P, SLOTS], U8, name="slot_scales_last", align_bytes=64)
        routed = keep.tile([P, T], F32, name="routed")
        nc.gpsimd.memset(token_scales[QUADRANT : 2 * QUADRANT, :].bitcast(I32), 0)
        nc.vector.memset(token_scales[2 * QUADRANT :, :].bitcast(I32), 0)
        nc.vector.memset(routed[:], 0.0)

        token_words = [keep.tile([P, T], U32, name="token_words%d" % o, align_bytes=ALIGN) for o in range(PASSES)]
        slot_words = {}
        bias = keep.tile([P, E + 1], F32, name="bias")
        gate_all = keep.tile([P, SLOTS], F32, name="gate_all")
        shared_sums = [psum_shared.tile([P, BANK], F32, name="shared_sums%d" % i) for i in range(T // BANK)]
        gate_row = keep.tile([P, GATE_RUN], F32, name="gate_row")
        w_codes = {}
        w_scales = {}
        banks = {}

        def place(shape, dtype, name, at, align=64):
            if at is None:
                return keep.tile(shape, dtype, name=name, align_bytes=align)
            if isinstance(at, str):
                return keep.tile(shape, dtype, name=name, tag=at, align_bytes=ALIGN)
            return turns.tile(shape, dtype, name=name, offset=at, align_bytes=ALIGN)

        def slot_offsets(first_expert, end_expert):
            return offsets[:, first_expert * C // PER_COLUMN : end_expert * C // PER_COLUMN]

        def load_tokens(o):
            nc.sync.dma_start(token_words[o][:].bitcast(I32), x_words[o].rearrange("p t r -> p (t r)").bitcast(I32))

        def gather_words(o, first_expert, end_expert, at=None):
            words = place([P, (end_expert - first_expert) * C], U32, "words%d_%d" % (o, first_expert), at)
            nc.vector.tensor_copy(words[:], token_words[o][:].indirect(slot_offsets(first_expert, end_expert)))
            for e in range(first_expert, end_expert):
                slot_words[e, o] = words[:, (e - first_expert) * C : (e - first_expert + 1) * C]

        def gather_scales():
            nc.sync.dma_start(token_scales[PACK * LAST : QUADRANT, :].bitcast(I32), x_scales[LAST].bitcast(I32))
            for q in range(P // QUADRANT):
                nc.sync.dma_start(
                    token_scales[QUADRANT * q : QUADRANT * q + PACK * LAST, :].bitcast(I32),
                    x_scales[:LAST, PACK * q : PACK * (q + 1), :].bitcast(I32),
                )
                if q == 0:
                    nc.sync.dma_start(gate_row[:], gate[0].rearrange("(p m) -> p m", m=GATE_RUN))
            nc.vector.tensor_copy(slot_scales[:], token_scales[:].indirect(offsets[:]))

        def shift_last_plane(target, source):
            for q in range(P // QUADRANT):
                rows = slice(PACK * (LAST + q), PACK * (LAST + q + 1))
                nc.sync.dma_start(target[QUADRANT * q : QUADRANT * q + PACK, :].bitcast(I32), source[rows, :].bitcast(I32))

        def spread_gate():
            identity = keep.tile([P, P], F32, name="identity")
            make_identity(nc, identity[:])
            by_run = gate_all[:].rearrange("q (p m) -> q p m", m=GATE_RUN)
            per_bank = BANK // P
            for m0 in range(0, GATE_RUN, per_bank):
                bank = psum_ring.tile([P, per_bank, P], F32, name="bank")
                for r in range(per_bank):
                    nc.tensor.transpose(bank[:, r, :], gate_row[:, m0 + r : m0 + r + 1].to_broadcast([P, P]), identity[:])
                nc.scalar.activation(by_run[:, :, m0 : m0 + per_bank], bank[:].rearrange("q r p -> q p r"), COPY)

        def load_weights(first, count, at=None):
            raw = place([P, count, PACK, N], F32, "raw%d" % first, at, ALIGN)
            rows = w_rows[first * K_PASS : (first + count) * K_PASS, :]
            nc.sync.dma_start(raw[:], rows.rearrange("(u p j) n -> p u j n", p=P, j=PACK))
            return raw

        def by_runs(copy):
            return lambda target, source: copy(
                target.rearrange("p u (c i) j -> p c u j i", i=4), source.rearrange("p u j (c i) -> p c u j i", i=4)
            )

        on_scalar = by_runs(nc.scalar.copy)
        on_vector = by_runs(nc.vector.tensor_copy)

        def on_gpsimd(target, source):
            nc.gpsimd.tensor_scalar(target, source.rearrange("p u j n -> p u n j"), 1.0, 0.0, MULT, ADD)

        def round_pieces(cast, first, raw, at=None):
            rounded = place([P, raw.shape[1], N, PACK], BF16, "rounded%d" % first, at)
            cast(rounded[:], raw)
            return rounded

        def quantize(pieces, rounded, at=None, scales_at=None):
            first, count = pieces[0], len(pieces)
            codes = place([P, count * N], U32, "codes%d" % first, at)
            scales = place([P, count * N], U8, "scales%d" % first, scales_at)
            nc.vector.quantize_mx(codes[:].bitcast(FP8X4), scales[:], rounded[:].rearrange("p u n j -> p (u n j)"))
            for u, piece in enumerate(pieces):
                w_codes[piece] = codes[:, u * N : (u + 1) * N]
                w_scales[piece] = scales[:, u * N : (u + 1) * N]

        def multiply(sums, piece, words, plane, start, stop):
            nc.tensor.matmul_mx(
                sums,
                lhsT=w_codes[piece].bitcast(FP8X4),
                lhsT_scale=w_scales[piece],
                rhs=words.bitcast(FP8X4),
                rhs_scale=plane,
                start=start,
                stop=stop,
            )

        def shared_passes(passes, first, last):
            for i in range(T // BANK):
                cols = slice(i * BANK, (i + 1) * BANK)
                for o in passes:
                    plane = token_scales[PACK * o :, cols] if o < LAST else token_scales_last[:, cols]
                    multiply(shared_sums[i][:], SHARED + o, token_words[o][:, cols], plane, o == first, o == last)

        def expert_product(e, order, part=slice(None)):
            slots = slice(e * C, (e + 1) * C)
            if e not in banks:
                bank = psum_ring.tile([P, BANK // P, P], F32, name="bank")
                banks[e] = bank[:].rearrange("q r p -> q (r p)")[:, :C]
            for o in order[part]:
                plane = slot_scales[PACK * o :, slots] if o < LAST else slot_scales_last[:, slots]
                multiply(banks[e], e * PASSES + o, slot_words[e, o], plane, o == order[0], o == order[-1])

        def expert_result(e, at=None, column=None):
            slots = slice(e * C, (e + 1) * C)
            y = place([P, C], F32, "y%d" % e, at)
            nc.vector.scalar_tensor_tensor(y[:], banks[e], bias[:, e : e + 1] if column is None else column, gate_all[:, slots], ADD, MULT)
            nc.scalar.activation(routed[:].indirect(slot_offsets(e, e + 1)), y[:], COPY)

        KIB = 1024
        nc.sync.dma_start(offsets[:], offs)
        gather_scales()
        load_tokens(0)
        gather_words(0, 0, E)
        load_tokens(1)
        gather_words(1, 0, E)
        raw = load_weights(SHARED, 2, "early0")
        spread_gate()
        hosts = [place([P, 2, N, PACK], BF16, "host%d" % o, None) for o in range(2)]
        for o in range(2):
            on_scalar(hosts[o][:, 1:], raw[:, o : o + 1])
        load_tokens(2)
        gather_words(2, 0, E)
        raw = load_weights(0, PASSES)
        quantize([0, 1], round_pieces(on_scalar, 0, raw[:, :2]))
        triple = round_pieces(on_scalar, 2, raw[:, 2:])
        nc.sync.dma_start(bias[:], b)
        own_bias = []
        for e, at in ((0, 0), (3, 15 * KIB)):
            own_bias.append(place([P, 8], F32, "own_bias%d" % e, at))
            nc.scalar.copy(own_bias[-1][:, :1], bias[:, e : e + 1])
        load_tokens(3)
        gather_words(3, 0, E)
        quantize([2, 3, 4], triple)
        quantize([5, 6], round_pieces(on_scalar, 5, load_weights(5, 2, "early1")[:]))
        quantize([7, 8, 9], round_pieces(on_scalar, 7, load_weights(7, 3)[:]))
        four = place([P, 4, N, PACK], BF16, "rounded10", "rounded10")
        on_scalar(four[:, :1], load_weights(10, 1)[:])
        for e in (0, 1):
            expert_product(e, range(PASSES), slice(LAST))
        load_tokens(LAST)
        shift_last_plane(slot_scales_last, slot_scales)
        gather_words(LAST, 0, 2)
        gather_words(LAST, 2, 4)
        for e in (0, 1):
            expert_product(e, range(PASSES), slice(LAST, None))
        on_scalar(four[:, 1:2], load_weights(11, 1)[:])
        on_scalar(four[:, 2:3], load_weights(12, 1, 2 * KIB)[:])
        on_scalar(four[:, 3:], load_weights(13, 1)[:])
        fifth = round_pieces(on_scalar, 14, load_weights(14, 1)[:])
        expert_result(0, 2 * KIB, own_bias[0][:, :1])
        between = [place([P, 2, N, PACK], BF16, "rounded15", 0)]
        on_scalar(between[0][:, :1], load_weights(15, 1)[:])
        gather_words(LAST, 4, E, 3 * KIB)
        quantize([10, 11, 12, 13], four)
        quantize([14], fifth)
        expert_product(2, range(PASSES))
        expert_result(1, "rounded10")
        raw = load_weights(16, 3, 5 * KIB)
        pair = round_pieces(on_vector, 16, raw[:, :2])
        on_vector(hosts[0][:, :1], raw[:, 2:])
        on_vector(between[0][:, 1:], load_weights(19, 1)[:])
        quantize([16, 17], pair)
        expert_result(2, 5 * KIB)
        quantize([15, 19], between[0])
        quantize([18, SHARED], hosts[0])
        expert_product(3, (1, 2, 0, 4, 3))
        shared_passes([0], 0, None)
        raw = load_weights(20, 3, "raw20")
        pair = round_pieces(on_vector, 20, raw[:, :2])
        pair2 = place([P, 2, N, PACK], BF16, "rounded22", None)
        on_vector(pair2[:, :1], raw[:, 2:])
        between.append(round_pieces(on_scalar, 25, load_weights(25, 1)[:]))
        raw = load_weights(23, 2)
        quantize([20, 21], pair)
        expert_result(3, "raw20", own_bias[1][:, :1])
        on_vector(pair2[:, 1:], raw[:, :1])
        on_vector(hosts[1][:, :1], raw[:, 1:])
        quantize([22, 23], pair2)
        quantize([24, SHARED + 1], hosts[1])
        expert_product(4, range(PASSES))
        shared_passes([1], 0, None)
        raw = load_weights(26, 2, 11 * KIB)
        single = round_pieces(on_vector, 26, raw[:, :1])
        pair = place([P, 2, N, PACK], BF16, "rounded27", None)
        on_vector(pair[:, :1], raw[:, 1:])
        late = place([P, 1, N, PACK], BF16, "rounded29", 15 * KIB)
        on_scalar(late[:], load_weights(29, 1)[:])
        raw28 = load_weights(28, 1, "early0")
        between.append(late)
        quantize([26], single)
        expert_result(4, 11 * KIB)
        on_vector(pair[:, 1:], raw28[:])
        quantize([25], between[1], 12 * KIB)
        quantize([27, 28], pair)
        quantize([29], between[2], "early0")
        expert_product(5, (1, 0, 2, 3, 4))
        third = round_pieces(on_vector, 32, load_weights(32, 1)[:])
        raw = load_weights(33, 2, "early1")
        last = [round_pieces(on_vector, 34, raw[:, 1:])]
        expert_result(E - 1)
        quantize([32], third)
        shared_passes([2], 0, None)
        last.append(round_pieces(on_vector, 33, raw[:, :1], "early0"))
        quantize([34], last[0])
        quantize([33], last[1])
        shift_last_plane(token_scales_last, token_scales)
        shared_passes([LAST, 3], 0, 3)

        starts = list(range(0, T, BANK)) + [T - BANK // 2, T]
        for start, end in zip(starts, starts[1:]):
            sums = shared_sums[start // BANK][:, start % BANK : start % BANK + end - start]
            result = keep.tile([P, end - start], F32, name="result%d" % start, align_bytes=ALIGN)
            nc.vector.scalar_tensor_tensor(result[:], sums, bias[:, E : E + 1], routed[:, start:end], ADD, ADD)
            nc.sync.dma_start(out[:, start:end], result[:])
